import numpy as np
import ml_dtypes


def mxq(x, axis, fmt="e4m3"):
    dtype, down = {"e4m3": (ml_dtypes.float8_e4m3fn, 7), "e5m2": (ml_dtypes.float8_e5m2, 14)}[fmt]
    v = np.moveaxis(np.asarray(x, np.float32).astype(ml_dtypes.bfloat16).astype(np.float64), axis, -1)
    blocks = v.reshape(v.shape[:-1] + (-1, 32))
    amax = np.abs(blocks).max(-1, keepdims=True)
    byte = np.maximum(np.where(amax > 0, np.frexp(amax)[1] - 1 + 127, 0) - down, 1)
    scale = np.exp2(byte - 127.0)
    codes = (blocks / scale).astype(np.float32).astype(dtype).astype(np.float64)
    return np.moveaxis((codes * scale).reshape(v.shape), -1, axis)


WIDE = False


def mx_kscale(k):
    if not WIDE:
        return np.ones(k)
    levels = np.array([10, -10, 5, -5, 0])
    if k % 512:
        return np.exp2(np.random.permutation(np.resize(levels, k // 32))).repeat(32)
    a = np.empty((k // 512, 16))
    for p in range(k // 512):
        a[p, :8] = np.random.permutation(np.resize(levels, 8))
        for g in range(8):
            far = levels[np.abs(levels - a[p, g]) >= 10]
            a[p, g + 8] = far[np.random.randint(len(far))]
    return np.exp2(a.ravel()).repeat(32)


def f64(x):
    return np.asarray(x).astype(np.float64)


def striped(idx):
    return np.tile(idx.reshape(-1, 16).T, (8, 1)).astype(np.uint16)


def unstriped(offs):
    return offs[:16].T.reshape(-1).astype(np.int64)


E2M1 = np.array([0.0, 0.5, 1.0, 1.5, 2.0, 3.0, 4.0, 6.0, -0.0, -0.5, -1.0, -1.5, -2.0, -3.0, -4.0, -6.0])


def pack_weight(w, fmt):
    k, n = w.shape
    w = f64(np.asarray(w, np.float32).astype(ml_dtypes.bfloat16)).reshape(k // 32, 32, n)
    amax = np.abs(w).max(1)
    if fmt == "e4m3":
        byte = np.frexp(amax)[1] - 1 + 127 - 7
    else:
        mant, ex = np.frexp(amax / 6.0)
        byte = np.where(mant > 0.5, ex, ex - 1) + 127
    byte = np.clip(np.where(amax > 0, byte, 1), 1, 254)
    scaled = (w * np.exp2(127.0 - byte)[:, None, :]).reshape(k, n).astype(np.float32)
    by_word = np.ascontiguousarray(scaled.reshape(k // 512, 128, 4, n).transpose(0, 1, 3, 2))
    if fmt == "e4m3":
        words = by_word.astype(ml_dtypes.float8_e4m3fn).view(np.uint8)
    else:
        c = by_word.astype(ml_dtypes.float4_e2m1fn).view(np.uint8) & 0xF
        words = (c[..., 0::2] | (c[..., 1::2] << 4)).reshape(k // 512, 128, 2 * n)
    return np.ascontiguousarray(words), np.ascontiguousarray(byte.astype(np.uint8).reshape(k // 512, 16, n))


def unpack_weight(words, scales, fmt):
    g, _, n = scales.shape
    words = np.ascontiguousarray(words).reshape(g, 128, n, -1)
    if fmt == "e4m3":
        vals = words.view(ml_dtypes.float8_e4m3fn).astype(np.float64)
    else:
        nib = np.empty((g, 128, n, 4), np.uint8)
        nib[..., 0::2] = words & 0xF
        nib[..., 1::2] = words >> 4
        vals = E2M1[nib]
    vals = vals * np.repeat(np.exp2(scales.astype(np.float64) - 127.0), 8, axis=1)[..., None]
    return vals.transpose(0, 1, 3, 2).reshape(g * 512, n)


def gelu(v):
    return 0.5 * v * (1.0 + np.tanh(np.sqrt(2.0 / np.pi) * (v + 0.044715 * v**3)))


K, H, T, S, T2, P = 1536, 1024, 2048, 512, 1024, 512

def setup_inputs():
    n = np.random.standard_normal
    s = mx_kscale(K)[:, None]
    u = mx_kscale(H)[:, None]
    d = {}
    d["tab_words"], d["tab_scales"] = pack_weight(n((K, T)) * s, "e4m3")
    d["offs"] = striped(np.random.permutation(T)[:S])
    d["wa"] = (n((K, H)) / K**0.5 / s * u.T).astype(np.float32)
    d["w4_words"], d["w4_scales"] = pack_weight(n((K, H)) / K**0.5 / s * u.T, "e2m1")
    d["gain"] = (0.6 * n(H)).astype(np.float32)
    d["wgs"] = np.exp(0.3 * n((128, S))).astype(np.float32)
    d["page0"] = (n((H, T2)) * u).astype(np.float32)
    d["offs2"] = striped(np.random.permutation(T2)[:S])
    d["offs3"] = striped(np.random.permutation(T2)[:P])
    d["base"] = (0.8 * n((H, P)) * u).astype(np.float32)
    d["metric"] = (n(H) / H**0.5 / u[:, 0]**2).astype(np.float32)
    d["slot"] = (0.9 * np.exp(0.3 * n(T2))).astype(np.float32)
    return d

def reference(tab_words, tab_scales, offs, wa, w4_words, w4_scales, gain, wgs, page0, offs2, offs3, base, metric, slot):
    v = unpack_weight(tab_words, tab_scales, "e4m3")[:, unstriped(offs)]
    ya = mxq(f64(wa), 0, "e4m3").T @ v
    yb = unpack_weight(w4_words, w4_scales, "e2m1").T @ v
    h = np.maximum(ya, yb) + f64(gain)[:, None] * np.minimum(ya, yb)
    page = f64(page0).copy()
    page[:, unstriped(offs2)] = np.tile(f64(wgs), (H // 128, 1)) * h
    x = (page[:, unstriped(offs3)] - f64(base)) * f64(metric)[:, None]
    e = mxq(page, 0, "e4m3").T @ mxq(x, 0, "e4m3")
    return np.tanh(f64(slot)[:, None] * e)

@@ -1,0 +1,426 @@
+from contextlib import ExitStack
+
+import concourse.mybir as mybir
+from concourse.masks import make_identity
+
+K, H, T, S, T2, NB = 1536, 1024, 2048, 512, 1024, 512
+FLOPS = 2 * (2 * K * H * S + H * T2 * NB)
+
+F32 = mybir.dt.float32
+BF16 = mybir.dt.bfloat16
+I32 = mybir.dt.int32
+U32 = mybir.dt.uint32
+U16 = mybir.dt.uint16
+U8 = mybir.dt.uint8
+FP8X4 = mybir.dt.float8_e4m3fn_x4
+FP4X4 = mybir.dt.float4_e2m1fn_x4
+ALU = mybir.AluOpType
+ACT = mybir.ActivationFunctionType
+
+P = 128
+PACK = 4
+KP = P * PACK
+KA = K // KP
+RB = H // KP
+JB = S // P
+MT = T2 // P
+
+
+def tile_list_perimetry_page_scores_kernel(
+    tc, tab_words, tab_scales, offs, wa, w4_words, w4_scales, gain, wgs, page0, offs2, offs3, base, metric, slot, out
+):
+    nc = tc.nc
+    with ExitStack() as ctx:
+        lists = ctx.enter_context(tc.tile_pool(name="lists", bufs=1))
+        keep = ctx.enter_context(tc.tile_pool(name="keep", bufs=1))
+        ring = ctx.enter_context(tc.tile_pool(name="ring", bufs=1))
+        psum = ctx.enter_context(tc.psum_pool(name="psum", bufs=1))
+
+        def slab(shape, dtype, name):
+            return ring.tile(shape, dtype, name=name, tag="slab", bufs=4, align_bytes=64)
+
+        def half_slab(shape, dtype, name):
+            return ring.tile(shape, dtype, name=name, tag="half_slab", bufs=2, align_bytes=64)
+
+        def bank(index, name):
+            return psum.tile([P, 512], F32, name=name, tag="bank%d" % index)
+
+        idx = lists.tile([P, S // 16], U16, name="idx")
+        idx2 = lists.tile([P, S // 16], U16, name="idx2")
+        idx3 = lists.tile([P, NB // 16], U16, name="idx3")
+
+        tab_s = slab([P, KA * T], U8, "tab_s")
+        nc.vector.memset(tab_s[:].bitcast(I32), 0)
+        w4_s = keep.tile([P, KA, H], U8, name="w4_s", align_bytes=64)
+        nc.gpsimd.memset(w4_s[:].rearrange("p a n -> p (a n)").bitcast(I32), 0)
+        ident = keep.tile([P, P], F32, name="ident", align_bytes=64)
+        make_identity(nc, ident[:])
+
+        tab_w = [slab([P, T], I32, "tab_w%d" % a) for a in range(KA)]
+
+        def load_tab_w(a):
+            nc.sync.dma_start(out=tab_w[a][:], in_=tab_words[a].rearrange("p n t -> p (n t)").bitcast(I32))
+
+        nc.sync.dma_start(out=idx[:], in_=offs)
+        load_tab_w(0)
+        for q in range(4):
+            nc.scalar.dma_start(
+                out=tab_s[32 * q : 32 * q + 4, :].bitcast(I32).rearrange("r (a n) -> r a n", a=KA),
+                in_=tab_scales[:, 4 * q : 4 * q + 4, :].bitcast(I32).rearrange("a r n -> r a n"),
+            )
+        warm = keep.tile([P, 8], F32, name="warm")
+        nc.scalar.activation(warm[:, 0:1], ident[:, 0:1], ACT.Tanh)
+        load_tab_w(1)
+        load_tab_w(2)
+        w4_w = [keep.tile([P, KA, 2 * KP], U8, name="w4_w%d" % b, align_bytes=64) for b in range(RB)]
+
+        def load_w4(b):
+            nc.sync.dma_start(
+                out=w4_w[b][:].bitcast(I32),
+                in_=w4_words[:, :, 2 * KP * b : 2 * KP * (b + 1)].bitcast(I32).rearrange("a p n -> p a n"),
+            )
+
+        wa_raw = {}
+
+        def load_wa(b, a, c0=0, c1=KP):
+            wa_raw[b, a, c0] = ring.tile([P, PACK * (c1 - c0)], F32, name="wa_raw", tag="wa_raw", bufs=3, align_bytes=64)
+            nc.sync.dma_start(
+                out=wa_raw[b, a, c0][:].rearrange("p (t w) -> p t w", t=PACK),
+                in_=wa[KP * a : KP * (a + 1), KP * b + c0 : KP * b + c1].rearrange("(p j) w -> p j w", j=PACK),
+            )
+
+        page, base_t = {}, {}
+        page_rows = page0.rearrange("(b p t) m -> b t p m", p=P, t=PACK)
+        base_rows = base.rearrange("(b p t) j -> b t p j", p=P, t=PACK)
+
+        def load_page(n):
+            page[n] = ring.tile([P, T2], F32, name="page", tag="page", bufs=6)
+            nc.sync.dma_start(out=page[n][:], in_=page_rows[n // PACK, n % PACK])
+
+        def load_base(n):
+            base_t[n] = ring.tile([P, NB], F32, name="base_t", tag="base_t", bufs=4)
+            nc.sync.dma_start(out=base_t[n][:], in_=base_rows[n // PACK, n % PACK])
+
+        load_w4(0)
+        for q in range(4):
+            nc.sync.dma_start(
+                out=w4_s[32 * q : 32 * q + 4, :, :].bitcast(I32),
+                in_=w4_scales[:, 4 * q : 4 * q + 4, :].bitcast(I32).rearrange("a r n -> r a n"),
+            )
+        head_pieces = [(0, 0, KP), (1, 0, KP), (2, 0, KP // 2), (2, KP // 2, KP)]
+        for a, c0, c1 in head_pieces:
+            load_wa(0, a, c0, c1)
+        load_page(0)
+        gain_t = keep.tile([P, RB, PACK], F32, name="gain_t")
+        nc.sync.dma_start(out=gain_t[:], in_=gain.rearrange("(b p t) -> p b t", p=P, t=PACK))
+        nc.sync.dma_start(out=idx2[:], in_=offs2)
+        wg = keep.tile([P, PACK, S], F32, name="wg")
+        for q in range(4):
+            nc.sync.dma_start(out=wg[32 * q : 32 * q + 32, :, :], in_=wgs.rearrange("(p t) j -> p t j", t=PACK))
+        load_w4(1)
+        nc.sync.dma_start(out=idx3[:], in_=offs3)
+        load_base(0)
+        load_page(1)
+        metric_t = keep.tile([P, RB, PACK], F32, name="metric_t")
+        nc.sync.dma_start(out=metric_t[:], in_=metric.rearrange("(b p t) -> p b t", p=P, t=PACK))
+        load_wa(1, 0)
+        load_base(1)
+        load_wa(1, 1)
+        load_wa(1, 2)
+        slot_t = keep.tile([P, MT], F32, name="slot_t")
+        for n in range(2, RB * PACK):
+            load_page(n)
+            load_base(n)
+            if n == PACK:
+                with nc.allow_non_contiguous_dma(reason="one slot factor a partition"):
+                    nc.sync.dma_start(out=slot_t[:], in_=slot.rearrange("(i p) -> p i", p=P))
+
+        v_w = [keep.tile([P, S], U32, name="v_w%d" % a, align_bytes=64) for a in range(KA)]
+        v_s = [keep.tile([P, S], U8, name="v_s%d" % a, align_bytes=64) for a in range(KA)]
+        for a in range(KA):
+            nc.vector.tensor_copy(v_s[a][:], tab_s[:, T * a : T * (a + 1)].indirect(idx[:]))
+        for a in range(KA):
+            nc.vector.tensor_copy(v_w[a][:], tab_w[a][:].bitcast(U32).indirect(idx[:]))
+
+        yb_t, ybn_t, ya_t = {}, {}, {}
+
+        def dealt(acc):
+            return acc[:].rearrange("p (m t) -> p t m", t=PACK)
+
+        def product_b(b, banks):
+            for jb in range(JB):
+                acc = bank(banks[jb], "acc_b")
+                cols = slice(P * jb, P * (jb + 1))
+                for a in range(KA):
+                    nc.tensor.matmul_mx(
+                        out=acc[:],
+                        lhsT=v_w[a][:, cols].bitcast(FP8X4),
+                        lhsT_scale=v_s[a][:, cols],
+                        rhs=w4_w[b][:, a, :].bitcast(FP4X4),
+                        rhs_scale=w4_s[:, a, KP * b : KP * (b + 1)],
+                        start=(a == 0),
+                        stop=(a == KA - 1),
+                    )
+                yb_t[b, jb] = keep.tile([P, PACK, P], F32, name="yb_%d_%d" % (b, jb))
+                ybn_t[b, jb] = keep.tile([P, PACK, P], F32, name="ybn_%d_%d" % (b, jb))
+                nc.scalar.copy(yb_t[b, jb][:], dealt(acc))
+                nc.scalar.activation(ybn_t[b, jb][:], dealt(acc), ACT.Copy, scale=-1.0)
+
+        wa_c, wa_s, wa_bf = {}, {}, {}
+
+        def woven(dst, src):
+            return (
+                dst.rearrange("p (c i) t -> p c t i", i=4),
+                src.rearrange("p t (c i) -> p c t i", i=4),
+            )
+
+        def cast_wa(b, a, on_vector, c0=0, c1=KP):
+            wa_bf[b, a, c0] = half_slab([P, (c1 - c0) * PACK], BF16, "wa_bf")
+            dst, src = woven(
+                wa_bf[b, a, c0][:].rearrange("p (w t) -> p w t", t=PACK),
+                wa_raw[b, a, c0][:].rearrange("p (t w) -> p t w", t=PACK),
+            )
+            if on_vector:
+                nc.vector.tensor_copy(dst, src)
+            else:
+                nc.scalar.copy(dst, src)
+
+        def quant_wa(b, a, c0=0, c1=KP):
+            wa_c[b, a, c0] = ring.tile([P, c1 - c0], U32, name="wa_c", tag="wa_c", bufs=4, align_bytes=64)
+            wa_s[b, a, c0] = ring.tile([P, c1 - c0], U8, name="wa_s", tag="wa_s", bufs=4, align_bytes=64)
+            nc.vector.quantize_mx(
+                out=wa_c[b, a, c0][:].bitcast(FP8X4),
+                scales=wa_s[b, a, c0][:],
+                in_=wa_bf[b, a, c0][:],
+            )
+
+        acc_a = {}
+
+        def pass_a(b, a, c0=0, c1=KP):
+            for jb in range(JB):
+                if a == 0:
+                    acc_a[b, jb] = bank(jb, "acc_a")
+                cols = slice(P * jb, P * (jb + 1))
+                nc.tensor.matmul_mx(
+                    out=acc_a[b, jb][:, c0:c1],
+                    lhsT=v_w[a][:, cols].bitcast(FP8X4),
+                    lhsT_scale=v_s[a][:, cols],
+                    rhs=wa_c[b, a, c0][:].bitcast(FP8X4),
+                    rhs_scale=wa_s[b, a, c0][:],
+                    start=(a == 0),
+                    stop=(a == KA - 1 and c1 == KP),
+                )
+
+        def drain_a(b, t0, t1, shared):
+            for jb in range(JB):
+                if t0 == 0:
+                    ya_t[b, jb] = keep.tile([P, PACK, P], F32, name="ya_%d_%d" % (b, jb))
+                if shared and jb % 2 == 1:
+                    nc.vector.tensor_copy(ya_t[b, jb][:, t0:t1, :], dealt(acc_a[b, jb])[:, t0:t1, :])
+                else:
+                    nc.scalar.copy(ya_t[b, jb][:, t0:t1, :], dealt(acc_a[b, jb])[:, t0:t1, :])
+
+        product_b(0, [4, 5, 6, 7])
+        half_sum = keep.tile([P, RB * PACK], F32, name="half_sum")
+        half_dif = keep.tile([P, RB * PACK], F32, name="half_dif")
+        for a, c0, c1 in head_pieces:
+            cast_wa(0, a, True, c0, c1)
+            quant_wa(0, a, c0, c1)
+            pass_a(0, a, c0, c1)
+        gain_flat = gain_t[:].rearrange("p b t -> p (b t)")
+        nc.vector.tensor_scalar(half_sum[:], gain_flat, 0.5, 0.5, ALU.mult, ALU.add)
+        nc.vector.tensor_scalar(half_dif[:], gain_flat, -0.5, 0.5, ALU.mult, ALU.add)
+        drain_a(0, 0, 1, True)
+
+        parts, page_bf, x_bf = {}, {}, {}
+
+        def turn(n):
+            b, t = divmod(n, PACK)
+            dif = bank(4 + 2 * (n % 2), "dif")
+            tot = bank(5 + 2 * (n % 2), "tot")
+            for first in (True, False):
+                for acc, other in ((dif, ybn_t), (tot, yb_t)):
+                    for jb in range(JB):
+                        cols = slice(P * jb, P * (jb + 1))
+                        term = other if first == (t == 0) else ya_t
+                        nc.tensor.matmul(
+                            acc[:, cols],
+                            term[b, jb][:, t, :],
+                            ident[:],
+                            start=(first and jb == 0),
+                            stop=(not first and jb == JB - 1),
+                            is_transpose=True,
+                        )
+            if n == PACK:
+                page_bf[0] = slab([P, T2 * PACK], BF16, "page_bf")
+                gap = page_bf[0][:].bitcast(F32)[:, 0:S]
+                mid = wa_raw[1, KA - 1, 0][:, S : 2 * S]
+            else:
+                gap = ring.tile([P, S], F32, name="gap", tag="gap", bufs=2)[:]
+                mid = ring.tile([P, S], F32, name="mid", tag="mid", bufs=2)[:]
+            nc.scalar.activation(gap, dif[:], ACT.Abs)
+            if n == 0:
+                nc.vector.tensor_scalar(mid, tot[:], half_sum[:, n : n + 1], None, ALU.mult)
+            else:
+                nc.scalar.activation(mid, tot[:], ACT.Copy, scale=half_sum[:, n : n + 1])
+            parts[n] = (gap, mid)
+
+        h_t, comb, dev = {}, {}, {}
+
+        def combine(n):
+            gap, mid = parts[n]
+            if n == PACK - 1:
+                h_t[n] = wa_bf[1, KA - 1, 0][:].bitcast(F32)[:, 0:S]
+            elif n == PACK:
+                h_t[n] = page_bf[0][:].bitcast(F32)[:, 2 * S : 3 * S]
+            else:
+                h_t[n] = ring.tile([P, S], F32, name="h_t", tag="h_t", bufs=2)[:]
+            nc.vector.scalar_tensor_tensor(h_t[n], gap, half_dif[:, n : n + 1], mid, ALU.mult, ALU.add)
+
+        def put(n):
+            b, t = divmod(n, PACK)
+            nc.vector.tensor_tensor(page[n][:].indirect(idx2[:]), h_t[n], wg[:, t, :], ALU.mult)
+            if t == 0:
+                comb[b] = ring.tile([P, PACK, T2], F32, name="comb", tag="comb", bufs=1)
+            if n < RB * PACK - 1:
+                nc.gpsimd.dma_start(out=comb[b][:, t, :], in_=page[n][:])
+
+        x_rows = {}
+
+        def fetch(n):
+            b, t = divmod(n, PACK)
+            if t == 0:
+                dev[b] = slab([P, PACK, NB], F32, "dev")
+            nc.vector.tensor_tensor(dev[b][:, t, :], page[n][:].indirect(idx3[:]), base_t[n][:], ALU.subtract)
+
+        def scale_x(n):
+            b, t = divmod(n, PACK)
+            if n == 0:
+                x_rows[b] = wa_raw[1, KA - 1, 0][:].bitcast(BF16)[:, 0 : PACK * NB].rearrange("p (t j) -> p t j", t=PACK)
+            elif t == 0:
+                x_rows[b] = keep.tile([P, PACK, NB], BF16, name="x_rows")[:]
+            if n < RB * PACK - 1:
+                nc.scalar.activation(x_rows[b][:, t, :], dev[b][:, t, :], ACT.Copy, scale=metric_t[:, b, t : t + 1])
+            else:
+                nc.vector.tensor_scalar(x_rows[b][:, t, :], dev[b][:, t, :], metric_t[:, b, t : t + 1], None, ALU.mult)
+
+        page_c = [keep.tile([P, T2], U32, name="page_c%d" % b, align_bytes=64) for b in range(RB)]
+        page_s = [keep.tile([P, T2], U8, name="page_s%d" % b, align_bytes=64) for b in range(RB)]
+        x_c = [keep.tile([P, NB], U32, name="x_c%d" % b, align_bytes=64) for b in range(RB)]
+        x_s = [keep.tile([P, NB], U8, name="x_s%d" % b, align_bytes=64) for b in range(RB)]
+
+        def weave_page(b, t0=0, t1=PACK, halves=(0, 1)):
+            if t0 == 0 and b == 1:
+                page_bf[b] = slab([P, T2 * PACK], BF16, "page_bf")
+            for u in halves:
+                cols = slice(512 * u, 512 * (u + 1))
+                if b == RB - 1 and t1 == PACK:
+                    nc.scalar.copy(comb[b][:, PACK - 1, cols], page[RB * PACK - 1][:, cols])
+                dst, src = woven(page_bf[b][:].rearrange("p (m t) -> p m t", t=PACK)[:, cols, t0:t1], comb[b][:, t0:t1, cols])
+                nc.scalar.copy(dst, src)
+
+        def quant_page(b, halves=(0, 1)):
+            for u in halves:
+                cols = slice(512 * u, 512 * (u + 1))
+                nc.vector.quantize_mx(
+                    out=page_c[b][:, cols].bitcast(FP8X4),
+                    scales=page_s[b][:, cols],
+                    in_=page_bf[b][:, 2048 * u : 2048 * (u + 1)],
+                )
+
+        def weave_x(b, t0=0, t1=PACK):
+            if t0 == 0:
+                x_bf[b] = half_slab([P, NB, PACK], BF16, "x_bf")
+            dst, src = woven(x_bf[b][:, :, t0:t1], x_rows[b][:, t0:t1, :])
+            if t0 == 0:
+                nc.scalar.copy(dst, src)
+            else:
+                nc.vector.tensor_copy(dst, src)
+
+        def quant_x(b):
+            nc.vector.quantize_mx(
+                out=x_c[b][:].bitcast(FP8X4), scales=x_s[b][:], in_=x_bf[b][:].rearrange("p w t -> p (w t)")
+            )
+
+        turn(0)
+        combine(0)
+        drain_a(0, 1, PACK, False)
+        turn(1)
+        product_b(1, [0, 1, 2, 3])
+        put(0)
+        combine(1)
+        turn(2)
+        cast_wa(1, 0, False)
+        fetch(0)
+        quant_wa(1, 0)
+        pass_a(1, 0)
+        put(1)
+        combine(2)
+        cast_wa(1, 1, False)
+        turn(3)
+        fetch(1)
+        quant_wa(1, 1)
+        pass_a(1, 1)
+        cast_wa(1, 2, False)
+        put(2)
+        quant_wa(1, 2)
+        pass_a(1, 2)
+        drain_a(1, 0, 1, False)
+        turn(4)
+        drain_a(1, 1, PACK, False)
+        scale_x(0)
+        scale_x(1)
+        combine(3)
+        fetch(2)
+        put(3)
+        turn(5)
+        fetch(3)
+        combine(4)
+        put(4)
+        combine(5)
+        turn(6)
+        scale_x(2)
+        scale_x(3)
+        weave_page(0, halves=(0,))
+        fetch(4)
+        weave_page(0, halves=(1,))
+        put(5)
+        quant_page(0, halves=(0,))
+        combine(6)
+        turn(7)
+        weave_x(0)
+        scale_x(4)
+        fetch(5)
+        scale_x(5)
+        quant_page(0, halves=(1,))
+        put(6)
+        weave_page(1, 0, 2)
+        weave_x(1, 0, 2)
+        quant_x(0)
+        combine(7)
+        fetch(6)
+        scale_x(6)
+        put(7)
+        weave_page(1, 2, PACK)
+        fetch(7)
+        scale_x(7)
+        weave_x(1, 2, PACK)
+        quant_x(1)
+        quant_page(1)
+
+        for i in range(MT):
+            acc = bank(i, "score")
+            cols = slice(P * i, P * (i + 1))
+            for b in range(RB):
+                nc.tensor.matmul_mx(
+                    out=acc[:],
+                    lhsT=page_c[b][:, cols].bitcast(FP8X4),
+                    lhsT_scale=page_s[b][:, cols],
+                    rhs=x_c[b][:].bitcast(FP8X4),
+                    rhs_scale=x_s[b][:],
+                    start=(b == 0),
+                    stop=(b == RB - 1),
+                )
+            res = ring.tile([P, NB], F32, name="res", tag="page", bufs=6)
+            nc.scalar.activation(res[:], acc[:], ACT.Tanh, scale=slot_t[:, i : i + 1])
+            nc.sync.dma_start(out=out[cols, :], in_=res[:])

@@ -61,17 +61,6 @@ def tile_list_perimetry_page_scores_kernel(
         def load_tab_w(a):
             nc.sync.dma_start(out=tab_w[a][:], in_=tab_words[a].rearrange("p n t -> p (n t)").bitcast(I32))
 
-        nc.sync.dma_start(out=idx[:], in_=offs)
-        load_tab_w(0)
-        for q in range(4):
-            nc.scalar.dma_start(
-                out=tab_s[32 * q : 32 * q + 4, :].bitcast(I32).rearrange("r (a n) -> r a n", a=KA),
-                in_=tab_scales[:, 4 * q : 4 * q + 4, :].bitcast(I32).rearrange("a r n -> r a n"),
-            )
-        warm = keep.tile([P, 8], F32, name="warm")
-        nc.scalar.activation(warm[:, 0:1], ident[:, 0:1], ACT.Tanh)
-        load_tab_w(1)
-        load_tab_w(2)
         w4_w = [keep.tile([P, KA, 2 * KP], U8, name="w4_w%d" % b, align_bytes=64) for b in range(RB)]
 
         def load_w4(b):
@@ -80,12 +69,38 @@ def tile_list_perimetry_page_scores_kernel(
                 in_=w4_words[:, :, 2 * KP * b : 2 * KP * (b + 1)].bitcast(I32).rearrange("a p n -> p a n"),
             )
 
+        nc.sync.dma_start(out=idx[:], in_=offs)
+        load_w4(0)
+        for q in range(4):
+            nc.sync.dma_start(
+                out=tab_s[32 * q : 32 * q + 4, :].bitcast(I32).rearrange("r (a n) -> r a n", a=KA),
+                in_=tab_scales[:, 4 * q : 4 * q + 4, :].bitcast(I32).rearrange("a r n -> r a n"),
+            )
+        warm = keep.tile([P, 8], F32, name="warm")
+        nc.scalar.activation(warm[:, 0:1], ident[:, 0:1], ACT.Tanh)
+        load_tab_w(0)
+        load_tab_w(1)
+        for q in range(4):
+            nc.sync.dma_start(
+                out=w4_s[32 * q : 32 * q + 4, :, :].bitcast(I32),
+                in_=w4_scales[:, 4 * q : 4 * q + 4, :].bitcast(I32).rearrange("a r n -> r a n"),
+            )
+        load_tab_w(2)
+
         wa_raw = {}
+        comb = keep.tile([P, PACK * T2], F32, name="comb", align_bytes=64)
+        comb_rows = comb[:].rearrange("p (t m) -> p t m", t=PACK)
 
         def load_wa(b, a, c0=0, c1=KP):
-            wa_raw[b, a, c0] = ring.tile([P, PACK * (c1 - c0)], F32, name="wa_raw", tag="wa_raw", bufs=3, align_bytes=64)
+            if b == 1 and a != 1:
+                wa_raw[b, a, c0] = comb[:, PACK * KP * (a // 2) : PACK * KP * (a // 2 + 1)]
+            elif c0 == 0:
+                whole = ring.tile([P, PACK * KP], F32, name="wa_raw", tag="wa_raw", bufs=3, align_bytes=64)
+                wa_raw[b, a, 0] = whole[:, 0 : PACK * c1]
+                if c1 < KP:
+                    wa_raw[b, a, c1] = whole[:, PACK * c1 : PACK * KP]
             nc.sync.dma_start(
-                out=wa_raw[b, a, c0][:].rearrange("p (t w) -> p t w", t=PACK),
+                out=wa_raw[b, a, c0].rearrange("p (t w) -> p t w", t=PACK),
                 in_=wa[KP * a : KP * (a + 1), KP * b + c0 : KP * b + c1].rearrange("(p j) w -> p j w", j=PACK),
             )
 
@@ -98,38 +113,41 @@ def tile_list_perimetry_page_scores_kernel(
             nc.sync.dma_start(out=page[n][:], in_=page_rows[n // PACK, n % PACK])
 
         def load_base(n):
-            base_t[n] = ring.tile([P, NB], F32, name="base_t", tag="base_t", bufs=4)
+            base_t[n] = ring.tile([P, NB], F32, name="base_t", tag="base_t", bufs=8)
             nc.sync.dma_start(out=base_t[n][:], in_=base_rows[n // PACK, n % PACK])
 
-        load_w4(0)
-        for q in range(4):
-            nc.sync.dma_start(
-                out=w4_s[32 * q : 32 * q + 4, :, :].bitcast(I32),
-                in_=w4_scales[:, 4 * q : 4 * q + 4, :].bitcast(I32).rearrange("a r n -> r a n"),
-            )
-        head_pieces = [(0, 0, KP), (1, 0, KP), (2, 0, KP // 2), (2, KP // 2, KP)]
-        for a, c0, c1 in head_pieces:
-            load_wa(0, a, c0, c1)
+        for a in range(KA):
+            load_wa(0, a)
         load_page(0)
         gain_t = keep.tile([P, RB, PACK], F32, name="gain_t")
         nc.sync.dma_start(out=gain_t[:], in_=gain.rearrange("(b p t) -> p b t", p=P, t=PACK))
         nc.sync.dma_start(out=idx2[:], in_=offs2)
-        wg = keep.tile([P, PACK, S], F32, name="wg")
-        for q in range(4):
-            nc.sync.dma_start(out=wg[32 * q : 32 * q + 32, :, :], in_=wgs.rearrange("(p t) j -> p t j", t=PACK))
+        wg = [keep.tile([P, 2, S], F32, name="wg%d" % u) for u in range(2)]
+
+        def load_wg(u):
+            for q in range(4):
+                nc.sync.dma_start(
+                    out=wg[u][32 * q : 32 * q + 32, :, :],
+                    in_=wgs.rearrange("(p t) j -> p t j", t=PACK)[:, 2 * u : 2 * u + 2, :],
+                )
+
+        load_wg(0)
         load_w4(1)
+        load_page(1)
         nc.sync.dma_start(out=idx3[:], in_=offs3)
         load_base(0)
-        load_page(1)
         metric_t = keep.tile([P, RB, PACK], F32, name="metric_t")
         nc.sync.dma_start(out=metric_t[:], in_=metric.rearrange("(b p t) -> p b t", p=P, t=PACK))
         load_wa(1, 0)
-        load_base(1)
+        load_wg(1)
         load_wa(1, 1)
+        load_page(2)
+        load_base(1)
         load_wa(1, 2)
         slot_t = keep.tile([P, MT], F32, name="slot_t")
         for n in range(2, RB * PACK):
-            load_page(n)
+            if n > 2:
+                load_page(n)
             load_base(n)
             if n == PACK:
                 with nc.allow_non_contiguous_dma(reason="one slot factor a partition"):
@@ -148,12 +166,15 @@ def tile_list_perimetry_page_scores_kernel(
             return acc[:].rearrange("p (m t) -> p t m", t=PACK)
 
         def product_b(b, banks):
-            for jb in range(JB):
-                acc = bank(banks[jb], "acc_b")
-                cols = slice(P * jb, P * (jb + 1))
-                for a in range(KA):
+            accs = [bank(banks[jb], "acc_b") for jb in range(JB)]
+            order = [(a, jb) for a in range(KA) for jb in range(JB)]
+            if b == 1:
+                order = [(a, jb) for jb in range(JB) for a in range(KA)]
+            for a, jb in order:
+                if True:
+                    cols = slice(P * jb, P * (jb + 1))
                     nc.tensor.matmul_mx(
-                        out=acc[:],
+                        out=accs[jb][:],
                         lhsT=v_w[a][:, cols].bitcast(FP8X4),
                         lhsT_scale=v_s[a][:, cols],
                         rhs=w4_w[b][:, a, :].bitcast(FP4X4),
@@ -161,10 +182,13 @@ def tile_list_perimetry_page_scores_kernel(
                         start=(a == 0),
                         stop=(a == KA - 1),
                     )
+            for jb in range(JB):
+                acc = accs[jb]
                 yb_t[b, jb] = keep.tile([P, PACK, P], F32, name="yb_%d_%d" % (b, jb))
                 ybn_t[b, jb] = keep.tile([P, PACK, P], F32, name="ybn_%d_%d" % (b, jb))
                 nc.scalar.copy(yb_t[b, jb][:], dealt(acc))
-                nc.scalar.activation(ybn_t[b, jb][:], dealt(acc), ACT.Copy, scale=-1.0)
+                t0 = 1 - b
+                nc.scalar.activation(ybn_t[b, jb][:, t0:PACK, :], dealt(acc)[:, t0:PACK, :], ACT.Copy, scale=-1.0)
 
         wa_c, wa_s, wa_bf = {}, {}, {}
 
@@ -178,7 +202,7 @@ def tile_list_perimetry_page_scores_kernel(
             wa_bf[b, a, c0] = half_slab([P, (c1 - c0) * PACK], BF16, "wa_bf")
             dst, src = woven(
                 wa_bf[b, a, c0][:].rearrange("p (w t) -> p w t", t=PACK),
-                wa_raw[b, a, c0][:].rearrange("p (t w) -> p t w", t=PACK),
+                wa_raw[b, a, c0].rearrange("p (t w) -> p t w", t=PACK),
             )
             if on_vector:
                 nc.vector.tensor_copy(dst, src)
@@ -186,7 +210,10 @@ def tile_list_perimetry_page_scores_kernel(
                 nc.scalar.copy(dst, src)
 
         def quant_wa(b, a, c0=0, c1=KP):
-            wa_c[b, a, c0] = ring.tile([P, c1 - c0], U32, name="wa_c", tag="wa_c", bufs=4, align_bytes=64)
+            if a < KA - 1:
+                wa_c[b, a, c0] = ring.tile([P, c1 - c0], U32, name="wa_c", tag="wa_c", bufs=4, align_bytes=64)
+            else:
+                wa_c[b, a, c0] = ring.tile([P, c1 - c0], U32, name="wa_c", tag="late", bufs=1, align_bytes=64)
             wa_s[b, a, c0] = ring.tile([P, c1 - c0], U8, name="wa_s", tag="wa_s", bufs=4, align_bytes=64)
             nc.vector.quantize_mx(
                 out=wa_c[b, a, c0][:].bitcast(FP8X4),
@@ -221,16 +248,86 @@ def tile_list_perimetry_page_scores_kernel(
                     nc.scalar.copy(ya_t[b, jb][:, t0:t1, :], dealt(acc_a[b, jb])[:, t0:t1, :])
 
         product_b(0, [4, 5, 6, 7])
+        yb_turned = bank(5, "yb_turned")
+        for jb in range(JB):
+            nc.tensor.transpose(yb_turned[:, P * jb : P * (jb + 1)], yb_t[0, jb][:, 0, :], ident[:])
+        yb_first = keep.tile([P, S], F32, name="yb_first")
+        nc.scalar.copy(yb_first[:], yb_turned[:])
+        ya_first = bank(4, "ya_first")
+
+        def cast_dealt(a, t0, t1):
+            if t0 == 0:
+                wa_bf[0, a, 0] = half_slab([P, KP * PACK], BF16, "wa_bf")
+                wa_c[0, a, 0] = ring.tile([P, KP], U32, name="wa_c", tag="wa_c", bufs=4, align_bytes=64)
+                wa_s[0, a, 0] = ring.tile([P, KP], U8, name="wa_s", tag="wa_s", bufs=4, align_bytes=64)
+            nc.vector.tensor_copy(
+                wa_bf[0, a, 0][:].rearrange("p (t m j) -> p m j t", t=PACK, j=PACK)[:, :, :, t0:t1],
+                wa_raw[0, a, 0].rearrange("p (j m t) -> p m j t", t=PACK, j=PACK)[:, :, :, t0:t1],
+            )
+
+        def quant_dealt(a, t0, t1):
+            nc.vector.quantize_mx(
+                out=wa_c[0, a, 0][:, P * t0 : P * t1].bitcast(FP8X4),
+                scales=wa_s[0, a, 0][:, P * t0 : P * t1],
+                in_=wa_bf[0, a, 0][:, KP * t0 : KP * t1],
+            )
+
+        def pass_first(a):
+            nc.tensor.matmul_mx(
+                out=ya_first[:],
+                lhsT=wa_c[0, a, 0][:, 0:P].bitcast(FP8X4),
+                lhsT_scale=wa_s[0, a, 0][:, 0:P],
+                rhs=v_w[a][:].bitcast(FP8X4),
+                rhs_scale=v_s[a][:],
+                start=(a == 0),
+                stop=(a == KA - 1),
+            )
+
+        def pass_rest(a):
+            for jb in range(JB):
+                if a == 0:
+                    acc_a[0, jb] = bank(jb, "acc_a")
+                cols = slice(P * jb, P * (jb + 1))
+                for t0, t1 in ((1, 3), (3, 4)):
+                    nc.tensor.matmul_mx(
+                        out=acc_a[0, jb][:, P * t0 : P * t1],
+                        lhsT=v_w[a][:, cols].bitcast(FP8X4),
+                        lhsT_scale=v_s[a][:, cols],
+                        rhs=wa_c[0, a, 0][:, P * t0 : P * t1].bitcast(FP8X4),
+                        rhs_scale=wa_s[0, a, 0][:, P * t0 : P * t1],
+                        start=(a == 0 and t0 == 1),
+                        stop=(a == KA - 1 and t1 == PACK),
+                    )
+
+        for a in range(KA - 1):
+            cast_dealt(a, 0, PACK)
+            quant_dealt(a, 0, PACK)
+            pass_rest(a)
+            pass_first(a)
+        last = KA - 1
+        cast_dealt(last, 0, 1)
+        quant_dealt(last, 0, 1)
+        pass_first(last)
+        cast_dealt(last, 1, PACK)
+        quant_dealt(last, 1, 3)
+        quant_dealt(last, 3, PACK)
+        pass_rest(last)
+        gain_flat = gain_t[:].rearrange("p b t -> p (b t)")
+        h_t, dev = {}, {}
+        h_row = keep.tile([P, S], F32, name="h_row")
+        high = ring.tile([P, S], F32, name="high", tag="gap", bufs=2)
+        low = ring.tile([P, S], F32, name="low", tag="mid", bufs=2)
+        nc.vector.tensor_tensor(high[:], ya_first[:], yb_first[:], ALU.max)
+        nc.vector.tensor_tensor(low[:], ya_first[:], yb_first[:], ALU.min)
         half_sum = keep.tile([P, RB * PACK], F32, name="half_sum")
         half_dif = keep.tile([P, RB * PACK], F32, name="half_dif")
-        for a, c0, c1 in head_pieces:
-            cast_wa(0, a, True, c0, c1)
-            quant_wa(0, a, c0, c1)
-            pass_a(0, a, c0, c1)
-        gain_flat = gain_t[:].rearrange("p b t -> p (b t)")
         nc.vector.tensor_scalar(half_sum[:], gain_flat, 0.5, 0.5, ALU.mult, ALU.add)
+        nc.vector.scalar_tensor_tensor(h_row[:], low[:], gain_flat[:, 0:1], high[:], ALU.mult, ALU.add)
         nc.vector.tensor_scalar(half_dif[:], gain_flat, -0.5, 0.5, ALU.mult, ALU.add)
-        drain_a(0, 0, 1, True)
+        h_t[0] = h_row[:]
+        for jb in range(JB):
+            ya_t[0, jb] = keep.tile([P, PACK, P], F32, name="ya_0_%d" % jb)
+            nc.scalar.copy(ya_t[0, jb][:, 1:PACK, :].rearrange("p t m -> p (t m)"), acc_a[0, jb][:, P:KP])
 
         parts, page_bf, x_bf = {}, {}, {}
 
@@ -242,7 +339,7 @@ def tile_list_perimetry_page_scores_kernel(
                 for acc, other in ((dif, ybn_t), (tot, yb_t)):
                     for jb in range(JB):
                         cols = slice(P * jb, P * (jb + 1))
-                        term = other if first == (t == 0) else ya_t
+                        term = other if first else ya_t
                         nc.tensor.matmul(
                             acc[:, cols],
                             term[b, jb][:, t, :],
@@ -254,36 +351,34 @@ def tile_list_perimetry_page_scores_kernel(
             if n == PACK:
                 page_bf[0] = slab([P, T2 * PACK], BF16, "page_bf")
                 gap = page_bf[0][:].bitcast(F32)[:, 0:S]
-                mid = wa_raw[1, KA - 1, 0][:, S : 2 * S]
+                mid = wa_raw[1, 1, 0][:, S : 2 * S]
             else:
-                gap = ring.tile([P, S], F32, name="gap", tag="gap", bufs=2)[:]
                 mid = ring.tile([P, S], F32, name="mid", tag="mid", bufs=2)[:]
+                if n == PACK + 1:
+                    gap = page_bf[0][:].bitcast(F32)[:, 2 * S : 3 * S]
+                else:
+                    gap = ring.tile([P, S], F32, name="gap", tag="gap", bufs=2)[:]
             nc.scalar.activation(gap, dif[:], ACT.Abs)
-            if n == 0:
-                nc.vector.tensor_scalar(mid, tot[:], half_sum[:, n : n + 1], None, ALU.mult)
-            else:
-                nc.scalar.activation(mid, tot[:], ACT.Copy, scale=half_sum[:, n : n + 1])
+            nc.scalar.activation(mid, tot[:], ACT.Copy, scale=half_sum[:, n : n + 1])
             parts[n] = (gap, mid)
-
-        h_t, comb, dev = {}, {}, {}
 
         def combine(n):
             gap, mid = parts[n]
-            if n == PACK - 1:
-                h_t[n] = wa_bf[1, KA - 1, 0][:].bitcast(F32)[:, 0:S]
-            elif n == PACK:
-                h_t[n] = page_bf[0][:].bitcast(F32)[:, 2 * S : 3 * S]
+            if n == 1:
+                h_t[n] = h_row[:]
+            elif n == 2:
+                h_t[n] = ring.tile([P, S], F32, name="h_two", tag="late", bufs=1, align_bytes=64)[:]
             else:
-                h_t[n] = ring.tile([P, S], F32, name="h_t", tag="h_t", bufs=2)[:]
+                h_t[n] = wa_bf[1, KA - 1, 0][:].bitcast(F32)[:, 0:S]
             nc.vector.scalar_tensor_tensor(h_t[n], gap, half_dif[:, n : n + 1], mid, ALU.mult, ALU.add)
 
         def put(n):
             b, t = divmod(n, PACK)
-            nc.vector.tensor_tensor(page[n][:].indirect(idx2[:]), h_t[n], wg[:, t, :], ALU.mult)
-            if t == 0:
-                comb[b] = ring.tile([P, PACK, T2], F32, name="comb", tag="comb", bufs=1)
-            if n < RB * PACK - 1:
-                nc.gpsimd.dma_start(out=comb[b][:, t, :], in_=page[n][:])
+            nc.vector.tensor_tensor(page[n][:].indirect(idx2[:]), h_t[n], wg[t // 2][:, t % 2, :], ALU.mult)
+
+        def join(n):
+            t = n % PACK
+            nc.gpsimd.dma_start(out=comb[:, T2 * t : T2 * (t + 1)], in_=page[n][:])
 
         x_rows = {}
 
@@ -296,7 +391,7 @@ def tile_list_perimetry_page_scores_kernel(
         def scale_x(n):
             b, t = divmod(n, PACK)
             if n == 0:
-                x_rows[b] = wa_raw[1, KA - 1, 0][:].bitcast(BF16)[:, 0 : PACK * NB].rearrange("p (t j) -> p t j", t=PACK)
+                x_rows[b] = wa_raw[1, 1, 0].bitcast(BF16)[:, 0 : PACK * NB].rearrange("p (t j) -> p t j", t=PACK)
             elif t == 0:
                 x_rows[b] = keep.tile([P, PACK, NB], BF16, name="x_rows")[:]
             if n < RB * PACK - 1:
@@ -315,8 +410,8 @@ def tile_list_perimetry_page_scores_kernel(
             for u in halves:
                 cols = slice(512 * u, 512 * (u + 1))
                 if b == RB - 1 and t1 == PACK:
-                    nc.scalar.copy(comb[b][:, PACK - 1, cols], page[RB * PACK - 1][:, cols])
-                dst, src = woven(page_bf[b][:].rearrange("p (m t) -> p m t", t=PACK)[:, cols, t0:t1], comb[b][:, t0:t1, cols])
+                    nc.scalar.copy(comb_rows[:, PACK - 1, cols], page[RB * PACK - 1][:, cols])
+                dst, src = woven(page_bf[b][:].rearrange("p (m t) -> p m t", t=PACK)[:, cols, t0:t1], comb_rows[:, t0:t1, cols])
                 nc.scalar.copy(dst, src)
 
         def quant_page(b, halves=(0, 1)):
@@ -342,12 +437,9 @@ def tile_list_perimetry_page_scores_kernel(
                 out=x_c[b][:].bitcast(FP8X4), scales=x_s[b][:], in_=x_bf[b][:].rearrange("p w t -> p (w t)")
             )
 
-        turn(0)
-        combine(0)
-        drain_a(0, 1, PACK, False)
+        put(0)
         turn(1)
         product_b(1, [0, 1, 2, 3])
-        put(0)
         combine(1)
         turn(2)
         cast_wa(1, 0, False)
@@ -356,7 +448,9 @@ def tile_list_perimetry_page_scores_kernel(
         pass_a(1, 0)
         put(1)
         combine(2)
+        join(0)
         cast_wa(1, 1, False)
+        join(1)
         turn(3)
         fetch(1)
         quant_wa(1, 1)
@@ -368,11 +462,13 @@ def tile_list_perimetry_page_scores_kernel(
         drain_a(1, 0, 1, False)
         turn(4)
         drain_a(1, 1, PACK, False)
+        join(2)
         scale_x(0)
         scale_x(1)
-        combine(3)
         fetch(2)
+        combine(3)
         put(3)
+        join(3)
         turn(5)
         fetch(3)
         combine(4)
@@ -384,19 +480,22 @@ def tile_list_perimetry_page_scores_kernel(
         weave_page(0, halves=(0,))
         fetch(4)
         weave_page(0, halves=(1,))
+        join(4)
         put(5)
         quant_page(0, halves=(0,))
         combine(6)
         turn(7)
         weave_x(0)
+        join(5)
         scale_x(4)
         fetch(5)
         scale_x(5)
         quant_page(0, halves=(1,))
         put(6)
+        join(6)
+        quant_x(0)
         weave_page(1, 0, 2)
         weave_x(1, 0, 2)
-        quant_x(0)
         combine(7)
         fetch(6)
         scale_x(6)
@@ -405,8 +504,9 @@ def tile_list_perimetry_page_scores_kernel(
         fetch(7)
         scale_x(7)
         weave_x(1, 2, PACK)
+        quant_page(1, halves=(0,))
         quant_x(1)
-        quant_page(1)
+        quant_page(1, halves=(1,))
 
         for i in range(MT):
             acc = bank(i, "score")

@@ -36,27 +36,30 @@ def tile_list_perimetry_page_scores_kernel(
         ring = ctx.enter_context(tc.tile_pool(name="ring", bufs=1))
         psum = ctx.enter_context(tc.psum_pool(name="psum", bufs=1))
 
-        def slab(shape, dtype, name):
-            return ring.tile(shape, dtype, name=name, tag="slab", bufs=4, align_bytes=64)
+        def slab(index, shape, dtype, name):
+            return ring.tile(shape, dtype, name=name, tag="slab%d" % index, align_bytes=64)
 
-        def half_slab(shape, dtype, name):
-            return ring.tile(shape, dtype, name=name, tag="half_slab", bufs=2, align_bytes=64)
+        banks8 = [psum.tile([P, 512], F32, name="bank%d" % index) for index in range(8)]
 
         def bank(index, name):
-            return psum.tile([P, 512], F32, name=name, tag="bank%d" % index)
+            return banks8[index]
+
+        woven_bf = [keep.tile([P, KP * PACK], BF16, name="woven_bf%d" % u, align_bytes=64) for u in range(3)]
+        gaps = [keep.tile([P, S], F32, name="gap%d" % u) for u in range(2)]
+        mids = [keep.tile([P, S], F32, name="mid%d" % u) for u in range(2)]
 
         idx = lists.tile([P, S // 16], U16, name="idx")
         idx2 = lists.tile([P, S // 16], U16, name="idx2")
         idx3 = lists.tile([P, NB // 16], U16, name="idx3")
 
-        tab_s = slab([P, KA * T], U8, "tab_s")
+        tab_s = slab(0, [P, KA * T], U8, "tab_s")
         nc.vector.memset(tab_s[:].bitcast(I32), 0)
         w4_s = keep.tile([P, KA, H], U8, name="w4_s", align_bytes=64)
         nc.gpsimd.memset(w4_s[:].rearrange("p a n -> p (a n)").bitcast(I32), 0)
         ident = keep.tile([P, P], F32, name="ident", align_bytes=64)
         make_identity(nc, ident[:])
 
-        tab_w = [slab([P, T], I32, "tab_w%d" % a) for a in range(KA)]
+        tab_w = [slab(1 + a, [P, T], I32, "tab_w%d" % a) for a in range(KA)]
 
         def load_tab_w(a):
             nc.sync.dma_start(out=tab_w[a][:], in_=tab_words[a].rearrange("p n t -> p (n t)").bitcast(I32))
@@ -85,17 +88,16 @@ def tile_list_perimetry_page_scores_kernel(
                 out=w4_s[32 * q : 32 * q + 4, :, :].bitcast(I32),
                 in_=w4_scales[:, 4 * q : 4 * q + 4, :].bitcast(I32).rearrange("a r n -> r a n"),
             )
-        load_tab_w(2)
 
         wa_raw = {}
         comb = keep.tile([P, PACK * T2], F32, name="comb", align_bytes=64)
         comb_rows = comb[:].rearrange("p (t m) -> p t m", t=PACK)
 
         def load_wa(b, a, c0=0, c1=KP):
-            if b == 1 and a != 1:
-                wa_raw[b, a, c0] = comb[:, PACK * KP * (a // 2) : PACK * KP * (a // 2 + 1)]
+            if b == 1 and a < 2:
+                wa_raw[b, a, c0] = comb[:, PACK * KP * a : PACK * KP * (a + 1)]
             elif c0 == 0:
-                whole = ring.tile([P, PACK * KP], F32, name="wa_raw", tag="wa_raw", bufs=3, align_bytes=64)
+                whole = ring.tile([P, PACK * KP], F32, name="wa_raw", tag="wa_raw%d" % (a - b), align_bytes=64)
                 wa_raw[b, a, 0] = whole[:, 0 : PACK * c1]
                 if c1 < KP:
                     wa_raw[b, a, c1] = whole[:, PACK * c1 : PACK * KP]
@@ -109,41 +111,42 @@ def tile_list_perimetry_page_scores_kernel(
         base_rows = base.rearrange("(b p t) j -> b t p j", p=P, t=PACK)
 
         def load_page(n):
-            page[n] = ring.tile([P, T2], F32, name="page", tag="page", bufs=6)
+            page[n] = ring.tile([P, T2], F32, name="page", tag="page%d" % (n % 6))
             nc.sync.dma_start(out=page[n][:], in_=page_rows[n // PACK, n % PACK])
 
         def load_base(n):
-            base_t[n] = ring.tile([P, NB], F32, name="base_t", tag="base_t", bufs=8)
+            base_t[n] = keep.tile([P, NB], F32, name="base%d" % n)
             nc.sync.dma_start(out=base_t[n][:], in_=base_rows[n // PACK, n % PACK])
 
         for a in range(KA):
             load_wa(0, a)
+            if a == 0:
+                load_tab_w(KA - 1)
         load_page(0)
         gain_t = keep.tile([P, RB, PACK], F32, name="gain_t")
         nc.sync.dma_start(out=gain_t[:], in_=gain.rearrange("(b p t) -> p b t", p=P, t=PACK))
         nc.sync.dma_start(out=idx2[:], in_=offs2)
-        wg = [keep.tile([P, 2, S], F32, name="wg%d" % u) for u in range(2)]
+        wg = keep.tile([P, PACK * S], F32, name="wg")
 
-        def load_wg(u):
+        def load_wg(t0, t1):
             for q in range(4):
                 nc.sync.dma_start(
-                    out=wg[u][32 * q : 32 * q + 32, :, :],
-                    in_=wgs.rearrange("(p t) j -> p t j", t=PACK)[:, 2 * u : 2 * u + 2, :],
+                    out=wg[32 * q : 32 * q + 32, S * t0 : S * t1],
+                    in_=wgs.rearrange("(p t) j -> p (t j)", t=PACK)[:, S * t0 : S * t1],
                 )
 
-        load_wg(0)
+        load_wg(0, 1)
         load_w4(1)
-        load_page(1)
         nc.sync.dma_start(out=idx3[:], in_=offs3)
         load_base(0)
+        load_page(1)
         metric_t = keep.tile([P, RB, PACK], F32, name="metric_t")
         nc.sync.dma_start(out=metric_t[:], in_=metric.rearrange("(b p t) -> p b t", p=P, t=PACK))
-        load_wa(1, 0)
-        load_wg(1)
-        load_wa(1, 1)
-        load_page(2)
+        load_wg(1, PACK)
         load_base(1)
-        load_wa(1, 2)
+        load_page(2)
+        for a in range(KA):
+            load_wa(1, a)
         slot_t = keep.tile([P, MT], F32, name="slot_t")
         for n in range(2, RB * PACK):
             if n > 2:
@@ -183,14 +186,19 @@ def tile_list_perimetry_page_scores_kernel(
                         stop=(a == KA - 1),
                     )
             for jb in range(JB):
-                acc = accs[jb]
                 yb_t[b, jb] = keep.tile([P, PACK, P], F32, name="yb_%d_%d" % (b, jb))
-                ybn_t[b, jb] = keep.tile([P, PACK, P], F32, name="ybn_%d_%d" % (b, jb))
-                nc.scalar.copy(yb_t[b, jb][:], dealt(acc))
-                t0 = 1 - b
-                nc.scalar.activation(ybn_t[b, jb][:, t0:PACK, :], dealt(acc)[:, t0:PACK, :], ACT.Copy, scale=-1.0)
+                nc.scalar.copy(yb_t[b, jb][:], dealt(accs[jb]))
+                if b == 1:
+                    negate_b(b, jb, dealt(accs[jb]))
+
+        def negate_b(b, jb, source):
+            t0 = 1 - b
+            ybn_t[b, jb] = keep.tile([P, PACK, P], F32, name="ybn_%d_%d" % (b, jb))
+            nc.scalar.activation(ybn_t[b, jb][:, t0:PACK, :], source[:, t0:PACK, :], ACT.Copy, scale=-1.0)
 
         wa_c, wa_s, wa_bf = {}, {}, {}
+        codes = [keep.tile([P, KP], U32, name="wa_c%d" % a, align_bytes=64) for a in range(KA)]
+        planes = [keep.tile([P, KP], U8, name="wa_s%d" % a, align_bytes=64) for a in range(KA)]
 
         def woven(dst, src):
             return (
@@ -199,9 +207,9 @@ def tile_list_perimetry_page_scores_kernel(
             )
 
         def cast_wa(b, a, on_vector, c0=0, c1=KP):
-            wa_bf[b, a, c0] = half_slab([P, (c1 - c0) * PACK], BF16, "wa_bf")
+            wa_bf[b, a, c0] = woven_bf[(a + b) % 2 if (b, a) != (1, 0) else 2][:, PACK * c0 : PACK * c1]
             dst, src = woven(
-                wa_bf[b, a, c0][:].rearrange("p (w t) -> p w t", t=PACK),
+                wa_bf[b, a, c0].rearrange("p (w t) -> p w t", t=PACK),
                 wa_raw[b, a, c0].rearrange("p (t w) -> p t w", t=PACK),
             )
             if on_vector:
@@ -210,16 +218,12 @@ def tile_list_perimetry_page_scores_kernel(
                 nc.scalar.copy(dst, src)
 
         def quant_wa(b, a, c0=0, c1=KP):
-            if a < KA - 1:
-                wa_c[b, a, c0] = ring.tile([P, c1 - c0], U32, name="wa_c", tag="wa_c", bufs=4, align_bytes=64)
+            if (b, a) == (1, KA - 1):
+                wa_c[b, a, c0] = ring.tile([P, KP], U32, name="wa_c", tag="late", bufs=1, align_bytes=64)[:]
             else:
-                wa_c[b, a, c0] = ring.tile([P, c1 - c0], U32, name="wa_c", tag="late", bufs=1, align_bytes=64)
-            wa_s[b, a, c0] = ring.tile([P, c1 - c0], U8, name="wa_s", tag="wa_s", bufs=4, align_bytes=64)
-            nc.vector.quantize_mx(
-                out=wa_c[b, a, c0][:].bitcast(FP8X4),
-                scales=wa_s[b, a, c0][:],
-                in_=wa_bf[b, a, c0][:],
-            )
+                wa_c[b, a, c0] = codes[a][:, c0:c1]
+            wa_s[b, a, c0] = planes[a][:, c0:c1]
+            nc.vector.quantize_mx(out=wa_c[b, a, c0].bitcast(FP8X4), scales=wa_s[b, a, c0], in_=wa_bf[b, a, c0])
 
         acc_a = {}
 
@@ -232,102 +236,90 @@ def tile_list_perimetry_page_scores_kernel(
                     out=acc_a[b, jb][:, c0:c1],
                     lhsT=v_w[a][:, cols].bitcast(FP8X4),
                     lhsT_scale=v_s[a][:, cols],
-                    rhs=wa_c[b, a, c0][:].bitcast(FP8X4),
-                    rhs_scale=wa_s[b, a, c0][:],
+                    rhs=wa_c[b, a, c0].bitcast(FP8X4),
+                    rhs_scale=wa_s[b, a, c0],
                     start=(a == 0),
                     stop=(a == KA - 1 and c1 == KP),
                 )
 
         def drain_a(b, t0, t1, shared):
             for jb in range(JB):
-                if t0 == 0:
+                if t0 == 1 - b:
                     ya_t[b, jb] = keep.tile([P, PACK, P], F32, name="ya_%d_%d" % (b, jb))
                 if shared and jb % 2 == 1:
                     nc.vector.tensor_copy(ya_t[b, jb][:, t0:t1, :], dealt(acc_a[b, jb])[:, t0:t1, :])
                 else:
                     nc.scalar.copy(ya_t[b, jb][:, t0:t1, :], dealt(acc_a[b, jb])[:, t0:t1, :])
 
+        cast_wa(0, 0, False)
         product_b(0, [4, 5, 6, 7])
         yb_turned = bank(5, "yb_turned")
         for jb in range(JB):
             nc.tensor.transpose(yb_turned[:, P * jb : P * (jb + 1)], yb_t[0, jb][:, 0, :], ident[:])
         yb_first = keep.tile([P, S], F32, name="yb_first")
         nc.scalar.copy(yb_first[:], yb_turned[:])
+        for jb in range(JB):
+            negate_b(0, jb, yb_t[0, jb])
         ya_first = bank(4, "ya_first")
 
-        def cast_dealt(a, t0, t1):
-            if t0 == 0:
-                wa_bf[0, a, 0] = half_slab([P, KP * PACK], BF16, "wa_bf")
-                wa_c[0, a, 0] = ring.tile([P, KP], U32, name="wa_c", tag="wa_c", bufs=4, align_bytes=64)
-                wa_s[0, a, 0] = ring.tile([P, KP], U8, name="wa_s", tag="wa_s", bufs=4, align_bytes=64)
-            nc.vector.tensor_copy(
-                wa_bf[0, a, 0][:].rearrange("p (t m j) -> p m j t", t=PACK, j=PACK)[:, :, :, t0:t1],
-                wa_raw[0, a, 0].rearrange("p (j m t) -> p m j t", t=PACK, j=PACK)[:, :, :, t0:t1],
-            )
+        first_c = keep.tile([P, KA * P], U32, name="first_c", align_bytes=64)
+        first_s = keep.tile([P, KA * P], U8, name="first_s", align_bytes=64)
+        for a in range(KA - 1):
+            nc.gpsimd.memset(planes[a][:].bitcast(I32), 0)
 
-        def quant_dealt(a, t0, t1):
-            nc.vector.quantize_mx(
-                out=wa_c[0, a, 0][:, P * t0 : P * t1].bitcast(FP8X4),
-                scales=wa_s[0, a, 0][:, P * t0 : P * t1],
-                in_=wa_bf[0, a, 0][:, KP * t0 : KP * t1],
-            )
+        def pick_first(a, c0, c1):
+            cols = slice(P * a + c0 // PACK, P * a + c1 // PACK)
+            nc.vector.tensor_copy(first_c[:, cols], codes[a][:, c0:c1:PACK])
+            nc.vector.tensor_copy(first_s[:, cols], planes[a][:, c0:c1:PACK])
 
         def pass_first(a):
+            cols = slice(P * a, P * (a + 1))
             nc.tensor.matmul_mx(
                 out=ya_first[:],
-                lhsT=wa_c[0, a, 0][:, 0:P].bitcast(FP8X4),
-                lhsT_scale=wa_s[0, a, 0][:, 0:P],
+                lhsT=first_c[:, cols].bitcast(FP8X4),
+                lhsT_scale=first_s[:, cols],
                 rhs=v_w[a][:].bitcast(FP8X4),
                 rhs_scale=v_s[a][:],
                 start=(a == 0),
                 stop=(a == KA - 1),
             )
 
-        def pass_rest(a):
-            for jb in range(JB):
-                if a == 0:
-                    acc_a[0, jb] = bank(jb, "acc_a")
-                cols = slice(P * jb, P * (jb + 1))
-                for t0, t1 in ((1, 3), (3, 4)):
-                    nc.tensor.matmul_mx(
-                        out=acc_a[0, jb][:, P * t0 : P * t1],
-                        lhsT=v_w[a][:, cols].bitcast(FP8X4),
-                        lhsT_scale=v_s[a][:, cols],
-                        rhs=wa_c[0, a, 0][:, P * t0 : P * t1].bitcast(FP8X4),
-                        rhs_scale=wa_s[0, a, 0][:, P * t0 : P * t1],
-                        start=(a == 0 and t0 == 1),
-                        stop=(a == KA - 1 and t1 == PACK),
-                    )
-
         for a in range(KA - 1):
-            cast_dealt(a, 0, PACK)
-            quant_dealt(a, 0, PACK)
-            pass_rest(a)
+            if a > 0:
+                cast_wa(0, a, True)
+            quant_wa(0, a)
+            pick_first(a, 0, KP)
             pass_first(a)
+            pass_a(0, a)
         last = KA - 1
-        cast_dealt(last, 0, 1)
-        quant_dealt(last, 0, 1)
+        first_bf = woven_bf[2][:, 0:KP]
+        nc.vector.tensor_copy(
+            first_bf.rearrange("p (m j) -> p m j", j=PACK),
+            wa_raw[0, last, 0].rearrange("p (j m t) -> p m j t", j=PACK, t=PACK)[:, :, :, 0],
+        )
+        nc.vector.quantize_mx(
+            out=first_c[:, P * last : P * KA].bitcast(FP8X4), scales=first_s[:, P * last : P * KA], in_=first_bf
+        )
         pass_first(last)
-        cast_dealt(last, 1, PACK)
-        quant_dealt(last, 1, 3)
-        quant_dealt(last, 3, PACK)
-        pass_rest(last)
+        cast_wa(0, last, True)
+        quant_wa(0, last)
+        pass_a(0, last)
         gain_flat = gain_t[:].rearrange("p b t -> p (b t)")
         h_t, dev = {}, {}
-        h_row = keep.tile([P, S], F32, name="h_row")
-        high = ring.tile([P, S], F32, name="high", tag="gap", bufs=2)
-        low = ring.tile([P, S], F32, name="low", tag="mid", bufs=2)
-        nc.vector.tensor_tensor(high[:], ya_first[:], yb_first[:], ALU.max)
-        nc.vector.tensor_tensor(low[:], ya_first[:], yb_first[:], ALU.min)
-        half_sum = keep.tile([P, RB * PACK], F32, name="half_sum")
+        h_row = ring.tile([P, S], F32, name="h_row", tag="late", bufs=1, align_bytes=64)
+        high = wa_raw[0, 0, 0][:, 0:S]
+        low = wa_raw[0, 0, 0][:, S : 2 * S]
+        nc.vector.tensor_tensor(high, ya_first[:], yb_first[:], ALU.max)
+        nc.vector.tensor_tensor(low, ya_first[:], yb_first[:], ALU.min)
+        dev[0] = slab(0, [P, PACK, NB], F32, "dev0")
+        dev[1] = slab(1, [P, PACK, NB], F32, "dev1")
         half_dif = keep.tile([P, RB * PACK], F32, name="half_dif")
-        nc.vector.tensor_scalar(half_sum[:], gain_flat, 0.5, 0.5, ALU.mult, ALU.add)
-        nc.vector.scalar_tensor_tensor(h_row[:], low[:], gain_flat[:, 0:1], high[:], ALU.mult, ALU.add)
+        nc.vector.tensor_scalar(dev[0][:, :, 0], gain_flat[:, 1:5], 0.5, 0.5, ALU.mult, ALU.add)
+        nc.vector.tensor_scalar(dev[1][:, 0:3, 0], gain_flat[:, 5:8], 0.5, 0.5, ALU.mult, ALU.add)
+        nc.vector.scalar_tensor_tensor(h_row[:], low, gain_flat[:, 0:1], high, ALU.mult, ALU.add)
         nc.vector.tensor_scalar(half_dif[:], gain_flat, -0.5, 0.5, ALU.mult, ALU.add)
         h_t[0] = h_row[:]
-        for jb in range(JB):
-            ya_t[0, jb] = keep.tile([P, PACK, P], F32, name="ya_0_%d" % jb)
-            nc.scalar.copy(ya_t[0, jb][:, 1:PACK, :].rearrange("p t m -> p (t m)"), acc_a[0, jb][:, P:KP])
+        drain_a(0, 1, PACK, False)
 
         parts, page_bf, x_bf = {}, {}, {}
 
@@ -339,7 +331,7 @@ def tile_list_perimetry_page_scores_kernel(
                 for acc, other in ((dif, ybn_t), (tot, yb_t)):
                     for jb in range(JB):
                         cols = slice(P * jb, P * (jb + 1))
-                        term = other if first else ya_t
+                        term = other if first == (n == PACK) else ya_t
                         nc.tensor.matmul(
                             acc[:, cols],
                             term[b, jb][:, t, :],
@@ -349,55 +341,61 @@ def tile_list_perimetry_page_scores_kernel(
                             is_transpose=True,
                         )
             if n == PACK:
-                page_bf[0] = slab([P, T2 * PACK], BF16, "page_bf")
+                page_bf[0] = slab(2, [P, T2 * PACK], BF16, "page_bf")
                 gap = page_bf[0][:].bitcast(F32)[:, 0:S]
-                mid = wa_raw[1, 1, 0][:, S : 2 * S]
+                mid = wa_raw[1, 2, 0][:, S : 2 * S]
             else:
-                mid = ring.tile([P, S], F32, name="mid", tag="mid", bufs=2)[:]
+                mid = mids[n % 2][:]
                 if n == PACK + 1:
                     gap = page_bf[0][:].bitcast(F32)[:, 2 * S : 3 * S]
                 else:
-                    gap = ring.tile([P, S], F32, name="gap", tag="gap", bufs=2)[:]
+                    gap = gaps[n % 2][:]
             nc.scalar.activation(gap, dif[:], ACT.Abs)
-            nc.scalar.activation(mid, tot[:], ACT.Copy, scale=half_sum[:, n : n + 1])
+            nc.scalar.activation(mid, tot[:], ACT.Copy, scale=dev[(n - 1) // PACK][:, (n - 1) % PACK, 0:1])
             parts[n] = (gap, mid)
 
         def combine(n):
             gap, mid = parts[n]
-            if n == 1:
-                h_t[n] = h_row[:]
-            elif n == 2:
+            if n < 3:
                 h_t[n] = ring.tile([P, S], F32, name="h_two", tag="late", bufs=1, align_bytes=64)[:]
+            elif n < 7:
+                h_t[n] = wa_bf[1, KA - 1, 0].bitcast(F32)[:, S * (n % 2) : S * (n % 2 + 1)]
             else:
-                h_t[n] = wa_bf[1, KA - 1, 0][:].bitcast(F32)[:, 0:S]
+                h_t[n] = page_bf[0][:].bitcast(F32)[:, 2 * S * (n - 6) : 2 * S * (n - 6) + S]
             nc.vector.scalar_tensor_tensor(h_t[n], gap, half_dif[:, n : n + 1], mid, ALU.mult, ALU.add)
 
         def put(n):
             b, t = divmod(n, PACK)
-            nc.vector.tensor_tensor(page[n][:].indirect(idx2[:]), h_t[n], wg[t // 2][:, t % 2, :], ALU.mult)
+            nc.vector.tensor_tensor(page[n][:].indirect(idx2[:]), h_t[n], wg[:, S * t : S * (t + 1)], ALU.mult)
+
+        def place(n):
+            return n if n < PACK else (1, 2, 0, 1)[n - PACK]
 
         def join(n):
-            t = n % PACK
-            nc.gpsimd.dma_start(out=comb[:, T2 * t : T2 * (t + 1)], in_=page[n][:])
+            t = place(n)
+            nc.sync.dma_start(out=comb[:, T2 * t : T2 * (t + 1)], in_=page[n][:])
 
-        x_rows = {}
-
-        def fetch(n):
+        def fetch(n, c0=0, c1=NB // 16):
             b, t = divmod(n, PACK)
-            if t == 0:
-                dev[b] = slab([P, PACK, NB], F32, "dev")
-            nc.vector.tensor_tensor(dev[b][:, t, :], page[n][:].indirect(idx3[:]), base_t[n][:], ALU.subtract)
+            cols = slice(16 * c0, 16 * c1)
+            nc.vector.tensor_tensor(
+                dev[b][:, t, cols], page[n][:].indirect(idx3[:, c0:c1]), base_t[n][:, cols], ALU.subtract
+            )
 
-        def scale_x(n):
-            b, t = divmod(n, PACK)
-            if n == 0:
-                x_rows[b] = wa_raw[1, 1, 0].bitcast(BF16)[:, 0 : PACK * NB].rearrange("p (t j) -> p t j", t=PACK)
-            elif t == 0:
-                x_rows[b] = keep.tile([P, PACK, NB], BF16, name="x_rows")[:]
-            if n < RB * PACK - 1:
-                nc.scalar.activation(x_rows[b][:, t, :], dev[b][:, t, :], ACT.Copy, scale=metric_t[:, b, t : t + 1])
+        def x_pair(b, u):
+            if b == 0:
+                host = wa_raw[1, 2, 0][:, NB * u : NB * (u + 1)]
             else:
-                nc.vector.tensor_scalar(x_rows[b][:, t, :], dev[b][:, t, :], metric_t[:, b, t : t + 1], None, ALU.mult)
+                host = comb[:, T2 * (3 - u) : T2 * (3 - u) + NB]
+            return host.bitcast(BF16).rearrange("p (t j) -> p t j", t=2)
+
+        def scale_x(n, cols=slice(0, NB)):
+            b, t = divmod(n, PACK)
+            row = x_pair(b, t // 2)[:, t % 2, cols]
+            if n < RB * PACK - 1:
+                nc.scalar.activation(row, dev[b][:, t, :], ACT.Copy, scale=metric_t[:, b, t : t + 1])
+            else:
+                nc.vector.tensor_scalar(row, dev[b][:, t, cols], metric_t[:, b, t : t + 1], None, ALU.mult)
 
         page_c = [keep.tile([P, T2], U32, name="page_c%d" % b, align_bytes=64) for b in range(RB)]
         page_s = [keep.tile([P, T2], U8, name="page_s%d" % b, align_bytes=64) for b in range(RB)]
@@ -406,12 +404,16 @@ def tile_list_perimetry_page_scores_kernel(
 
         def weave_page(b, t0=0, t1=PACK, halves=(0, 1)):
             if t0 == 0 and b == 1:
-                page_bf[b] = slab([P, T2 * PACK], BF16, "page_bf")
+                page_bf[b] = slab(3, [P, T2 * PACK], BF16, "page_bf")
             for u in halves:
                 cols = slice(512 * u, 512 * (u + 1))
                 if b == RB - 1 and t1 == PACK:
-                    nc.scalar.copy(comb_rows[:, PACK - 1, cols], page[RB * PACK - 1][:, cols])
-                dst, src = woven(page_bf[b][:].rearrange("p (m t) -> p m t", t=PACK)[:, cols, t0:t1], comb_rows[:, t0:t1, cols])
+                    nc.scalar.copy(comb_rows[:, place(RB * PACK - 1), cols], page[RB * PACK - 1][:, cols])
+                first = place(PACK * b + t0)
+                dst, src = woven(
+                    page_bf[b][:].rearrange("p (m t) -> p m t", t=PACK)[:, cols, t0:t1],
+                    comb_rows[:, first : first + t1 - t0, cols],
+                )
                 nc.scalar.copy(dst, src)
 
         def quant_page(b, halves=(0, 1)):
@@ -423,18 +425,24 @@ def tile_list_perimetry_page_scores_kernel(
                     in_=page_bf[b][:, 2048 * u : 2048 * (u + 1)],
                 )
 
-        def weave_x(b, t0=0, t1=PACK):
+        def weave_x(b, t0=0, t1=PACK, cols=slice(0, NB)):
             if t0 == 0:
-                x_bf[b] = half_slab([P, NB, PACK], BF16, "x_bf")
-            dst, src = woven(x_bf[b][:, :, t0:t1], x_rows[b][:, t0:t1, :])
+                x_bf[b] = woven_bf[b][:].rearrange("p (j t) -> p j t", t=PACK)
+            if b == 0:
+                rows = wa_raw[1, 2, 0][:, 0 : 2 * NB].bitcast(BF16).rearrange("p (t j) -> p t j", t=PACK)
+            else:
+                rows = x_pair(b, t0 // 2)
+            dst, src = woven(x_bf[b][:, cols, t0:t1], rows[:, :, cols])
             if t0 == 0:
                 nc.scalar.copy(dst, src)
             else:
                 nc.vector.tensor_copy(dst, src)
 
-        def quant_x(b):
+        def quant_x(b, cols=slice(0, NB)):
             nc.vector.quantize_mx(
-                out=x_c[b][:].bitcast(FP8X4), scales=x_s[b][:], in_=x_bf[b][:].rearrange("p w t -> p (w t)")
+                out=x_c[b][:, cols].bitcast(FP8X4),
+                scales=x_s[b][:, cols],
+                in_=x_bf[b][:, cols, :].rearrange("p w t -> p (w t)"),
             )
 
         put(0)
@@ -465,13 +473,13 @@ def tile_list_perimetry_page_scores_kernel(
         join(2)
         scale_x(0)
         scale_x(1)
-        fetch(2)
         combine(3)
+        fetch(2)
         put(3)
         join(3)
         turn(5)
-        fetch(3)
         combine(4)
+        fetch(3)
         put(4)
         combine(5)
         turn(6)
@@ -481,12 +489,12 @@ def tile_list_perimetry_page_scores_kernel(
         fetch(4)
         weave_page(0, halves=(1,))
         join(4)
-        put(5)
         quant_page(0, halves=(0,))
+        put(5)
+        join(5)
         combine(6)
         turn(7)
         weave_x(0)
-        join(5)
         scale_x(4)
         fetch(5)
         scale_x(5)
@@ -501,11 +509,16 @@ def tile_list_perimetry_page_scores_kernel(
         scale_x(6)
         put(7)
         weave_page(1, 2, PACK)
-        fetch(7)
-        scale_x(7)
-        weave_x(1, 2, PACK)
+        halves = (slice(0, NB // 2), slice(NB // 2, NB))
+        fetch(7, 0, 16)
+        fetch(7, 16, 32)
+        for cols in halves:
+            scale_x(7, cols)
+        for cols in halves:
+            weave_x(1, 2, PACK, cols)
+        for cols in halves:
+            quant_x(1, cols)
         quant_page(1, halves=(0,))
-        quant_x(1)
         quant_page(1, halves=(1,))
 
         for i in range(MT):
@@ -521,6 +534,6 @@ def tile_list_perimetry_page_scores_kernel(
                     start=(b == 0),
                     stop=(b == RB - 1),
                 )
-            res = ring.tile([P, NB], F32, name="res", tag="page", bufs=6)
+            res = base_t[i]
             nc.scalar.activation(res[:], acc[:], ACT.Tanh, scale=slot_t[:, i : i + 1])
             nc.sync.dma_start(out=out[cols, :], in_=res[:])

from contextlib import ExitStack

import concourse.mybir as mybir
from concourse.masks import make_identity

K, H, T, S, T2, NB = 1536, 1024, 2048, 512, 1024, 512
FLOPS = 2 * (2 * K * H * S + H * T2 * NB)

F32 = mybir.dt.float32
BF16 = mybir.dt.bfloat16
I32 = mybir.dt.int32
U32 = mybir.dt.uint32
U16 = mybir.dt.uint16
U8 = mybir.dt.uint8
FP8X4 = mybir.dt.float8_e4m3fn_x4
FP4X4 = mybir.dt.float4_e2m1fn_x4
ALU = mybir.AluOpType
ACT = mybir.ActivationFunctionType

P = 128
PACK = 4
KP = P * PACK
KA = K // KP
RB = H // KP
JB = S // P
MT = T2 // P


def tile_list_perimetry_page_scores_kernel(
    tc, tab_words, tab_scales, offs, wa, w4_words, w4_scales, gain, wgs, page0, offs2, offs3, base, metric, slot, out
):
    nc = tc.nc
    with ExitStack() as ctx:
        lists = ctx.enter_context(tc.tile_pool(name="lists", bufs=1))
        keep = ctx.enter_context(tc.tile_pool(name="keep", bufs=1))
        ring = ctx.enter_context(tc.tile_pool(name="ring", bufs=1))
        psum = ctx.enter_context(tc.psum_pool(name="psum", bufs=1))

        def slab(index, shape, dtype, name):
            return ring.tile(shape, dtype, name=name, tag="slab%d" % index, align_bytes=64)

        banks8 = [psum.tile([P, 512], F32, name="bank%d" % index) for index in range(8)]

        def bank(index, name):
            return banks8[index]

        woven_bf = [keep.tile([P, KP * PACK], BF16, name="woven_bf%d" % u, align_bytes=64) for u in range(3)]
        gaps = [keep.tile([P, S], F32, name="gap%d" % u) for u in range(2)]
        mids = [keep.tile([P, S], F32, name="mid%d" % u) for u in range(2)]

        idx = lists.tile([P, S // 16], U16, name="idx")
        idx2 = lists.tile([P, S // 16], U16, name="idx2")
        idx3 = lists.tile([P, NB // 16], U16, name="idx3")

        tab_s = slab(0, [P, KA * T], U8, "tab_s")
        nc.vector.memset(tab_s[:].bitcast(I32), 0)
        w4_s = keep.tile([P, KA, H], U8, name="w4_s", align_bytes=64)
        nc.gpsimd.memset(w4_s[:].rearrange("p a n -> p (a n)").bitcast(I32), 0)
        ident = keep.tile([P, P], F32, name="ident", align_bytes=64)
        make_identity(nc, ident[:])

        tab_w = [slab(1 + a, [P, T], I32, "tab_w%d" % a) for a in range(KA)]

        def load_tab_w(a):
            nc.sync.dma_start(out=tab_w[a][:], in_=tab_words[a].rearrange("p n t -> p (n t)").bitcast(I32))

        w4_w = [keep.tile([P, KA, 2 * KP], U8, name="w4_w%d" % b, align_bytes=64) for b in range(RB)]

        def load_w4(b):
            nc.sync.dma_start(
                out=w4_w[b][:].bitcast(I32),
                in_=w4_words[:, :, 2 * KP * b : 2 * KP * (b + 1)].bitcast(I32).rearrange("a p n -> p a n"),
            )

        nc.sync.dma_start(out=idx[:], in_=offs)
        load_w4(0)
        for q in range(4):
            nc.sync.dma_start(
                out=tab_s[32 * q : 32 * q + 4, :].bitcast(I32).rearrange("r (a n) -> r a n", a=KA),
                in_=tab_scales[:, 4 * q : 4 * q + 4, :].bitcast(I32).rearrange("a r n -> r a n"),
            )
        warm = keep.tile([P, 8], F32, name="warm")
        nc.scalar.activation(warm[:, 0:1], ident[:, 0:1], ACT.Tanh)
        load_tab_w(0)
        load_tab_w(1)
        for q in range(4):
            nc.sync.dma_start(
                out=w4_s[32 * q : 32 * q + 4, :, :].bitcast(I32),
                in_=w4_scales[:, 4 * q : 4 * q + 4, :].bitcast(I32).rearrange("a r n -> r a n"),
            )

        wa_raw = {}
        comb = keep.tile([P, PACK * T2], F32, name="comb", align_bytes=64)
        comb_rows = comb[:].rearrange("p (t m) -> p t m", t=PACK)

        def load_wa(b, a, c0=0, c1=KP):
            if b == 1 and a < 2:
                wa_raw[b, a, c0] = comb[:, PACK * KP * a : PACK * KP * (a + 1)]
            elif c0 == 0:
                whole = ring.tile([P, PACK * KP], F32, name="wa_raw", tag="wa_raw%d" % (a - b), align_bytes=64)
                wa_raw[b, a, 0] = whole[:, 0 : PACK * c1]
                if c1 < KP:
                    wa_raw[b, a, c1] = whole[:, PACK * c1 : PACK * KP]
            nc.sync.dma_start(
                out=wa_raw[b, a, c0].rearrange("p (t w) -> p t w", t=PACK),
                in_=wa[KP * a : KP * (a + 1), KP * b + c0 : KP * b + c1].rearrange("(p j) w -> p j w", j=PACK),
            )

        page, base_t = {}, {}
        page_rows = page0.rearrange("(b p t) m -> b t p m", p=P, t=PACK)
        base_rows = base.rearrange("(b p t) j -> b t p j", p=P, t=PACK)

        def load_page(n):
            page[n] = ring.tile([P, T2], F32, name="page", tag="page%d" % (n % 6))
            nc.sync.dma_start(out=page[n][:], in_=page_rows[n // PACK, n % PACK])

        def load_base(n):
            base_t[n] = keep.tile([P, NB], F32, name="base%d" % n)
            nc.sync.dma_start(out=base_t[n][:], in_=base_rows[n // PACK, n % PACK])

        for a in range(KA):
            load_wa(0, a)
            if a == 0:
                load_tab_w(KA - 1)
        load_page(0)
        gain_t = keep.tile([P, RB, PACK], F32, name="gain_t")
        nc.sync.dma_start(out=gain_t[:], in_=gain.rearrange("(b p t) -> p b t", p=P, t=PACK))
        nc.sync.dma_start(out=idx2[:], in_=offs2)
        wg = keep.tile([P, PACK * S], F32, name="wg")

        def load_wg(t0, t1):
            for q in range(4):
                nc.sync.dma_start(
                    out=wg[32 * q : 32 * q + 32, S * t0 : S * t1],
                    in_=wgs.rearrange("(p t) j -> p (t j)", t=PACK)[:, S * t0 : S * t1],
                )

        load_wg(0, 1)
        load_w4(1)
        nc.sync.dma_start(out=idx3[:], in_=offs3)
        load_base(0)
        load_page(1)
        metric_t = keep.tile([P, RB, PACK], F32, name="metric_t")
        nc.sync.dma_start(out=metric_t[:], in_=metric.rearrange("(b p t) -> p b t", p=P, t=PACK))
        load_wg(1, PACK)
        load_base(1)
        load_page(2)
        for a in range(KA):
            load_wa(1, a)
        slot_t = keep.tile([P, MT], F32, name="slot_t")
        for n in range(2, RB * PACK):
            if n > 2:
                load_page(n)
            load_base(n)
            if n == PACK:
                with nc.allow_non_contiguous_dma(reason="one slot factor a partition"):
                    nc.sync.dma_start(out=slot_t[:], in_=slot.rearrange("(i p) -> p i", p=P))

        v_w = [keep.tile([P, S], U32, name="v_w%d" % a, align_bytes=64) for a in range(KA)]
        v_s = [keep.tile([P, S], U8, name="v_s%d" % a, align_bytes=64) for a in range(KA)]
        for a in range(KA):
            nc.vector.tensor_copy(v_s[a][:], tab_s[:, T * a : T * (a + 1)].indirect(idx[:]))
        for a in range(KA):
            nc.vector.tensor_copy(v_w[a][:], tab_w[a][:].bitcast(U32).indirect(idx[:]))

        yb_t, ybn_t, ya_t = {}, {}, {}

        def dealt(acc):
            return acc[:].rearrange("p (m t) -> p t m", t=PACK)

        def product_b(b, banks):
            accs = [bank(banks[jb], "acc_b") for jb in range(JB)]
            order = [(a, jb) for a in range(KA) for jb in range(JB)]
            if b == 1:
                order = [(a, jb) for jb in range(JB) for a in range(KA)]
            for a, jb in order:
                if True:
                    cols = slice(P * jb, P * (jb + 1))
                    nc.tensor.matmul_mx(
                        out=accs[jb][:],
                        lhsT=v_w[a][:, cols].bitcast(FP8X4),
                        lhsT_scale=v_s[a][:, cols],
                        rhs=w4_w[b][:, a, :].bitcast(FP4X4),
                        rhs_scale=w4_s[:, a, KP * b : KP * (b + 1)],
                        start=(a == 0),
                        stop=(a == KA - 1),
                    )
            for jb in range(JB):
                yb_t[b, jb] = keep.tile([P, PACK, P], F32, name="yb_%d_%d" % (b, jb))
                nc.scalar.copy(yb_t[b, jb][:], dealt(accs[jb]))
                if b == 1:
                    negate_b(b, jb, dealt(accs[jb]))

        def negate_b(b, jb, source):
            t0 = 1 - b
            ybn_t[b, jb] = keep.tile([P, PACK, P], F32, name="ybn_%d_%d" % (b, jb))
            nc.scalar.activation(ybn_t[b, jb][:, t0:PACK, :], source[:, t0:PACK, :], ACT.Copy, scale=-1.0)

        wa_c, wa_s, wa_bf = {}, {}, {}
        codes = [keep.tile([P, KP], U32, name="wa_c%d" % a, align_bytes=64) for a in range(KA)]
        planes = [keep.tile([P, KP], U8, name="wa_s%d" % a, align_bytes=64) for a in range(KA)]

        def woven(dst, src):
            return (
                dst.rearrange("p (c i) t -> p c t i", i=4),
                src.rearrange("p t (c i) -> p c t i", i=4),
            )

        def cast_wa(b, a, on_vector, c0=0, c1=KP):
            wa_bf[b, a, c0] = woven_bf[(a + b) % 2 if (b, a) != (1, 0) else 2][:, PACK * c0 : PACK * c1]
            dst, src = woven(
                wa_bf[b, a, c0].rearrange("p (w t) -> p w t", t=PACK),
                wa_raw[b, a, c0].rearrange("p (t w) -> p t w", t=PACK),
            )
            if on_vector:
                nc.vector.tensor_copy(dst, src)
            else:
                nc.scalar.copy(dst, src)

        def quant_wa(b, a, c0=0, c1=KP):
            if (b, a) == (1, KA - 1):
                wa_c[b, a, c0] = ring.tile([P, KP], U32, name="wa_c", tag="late", bufs=1, align_bytes=64)[:]
            else:
                wa_c[b, a, c0] = codes[a][:, c0:c1]
            wa_s[b, a, c0] = planes[a][:, c0:c1]
            nc.vector.quantize_mx(out=wa_c[b, a, c0].bitcast(FP8X4), scales=wa_s[b, a, c0], in_=wa_bf[b, a, c0])

        acc_a = {}

        def pass_a(b, a, c0=0, c1=KP):
            for jb in range(JB):
                if a == 0:
                    acc_a[b, jb] = bank(jb, "acc_a")
                cols = slice(P * jb, P * (jb + 1))
                nc.tensor.matmul_mx(
                    out=acc_a[b, jb][:, c0:c1],
                    lhsT=v_w[a][:, cols].bitcast(FP8X4),
                    lhsT_scale=v_s[a][:, cols],
                    rhs=wa_c[b, a, c0].bitcast(FP8X4),
                    rhs_scale=wa_s[b, a, c0],
                    start=(a == 0),
                    stop=(a == KA - 1 and c1 == KP),
                )

        def drain_a(b, t0, t1, shared):
            for jb in range(JB):
                if t0 == 1 - b:
                    ya_t[b, jb] = keep.tile([P, PACK, P], F32, name="ya_%d_%d" % (b, jb))
                if shared and jb % 2 == 1:
                    nc.vector.tensor_copy(ya_t[b, jb][:, t0:t1, :], dealt(acc_a[b, jb])[:, t0:t1, :])
                else:
                    nc.scalar.copy(ya_t[b, jb][:, t0:t1, :], dealt(acc_a[b, jb])[:, t0:t1, :])

        cast_wa(0, 0, False)
        product_b(0, [4, 5, 6, 7])
        yb_turned = bank(5, "yb_turned")
        for jb in range(JB):
            nc.tensor.transpose(yb_turned[:, P * jb : P * (jb + 1)], yb_t[0, jb][:, 0, :], ident[:])
        yb_first = keep.tile([P, S], F32, name="yb_first")
        nc.scalar.copy(yb_first[:], yb_turned[:])
        for jb in range(JB):
            negate_b(0, jb, yb_t[0, jb])
        ya_first = bank(4, "ya_first")

        first_c = keep.tile([P, KA * P], U32, name="first_c", align_bytes=64)
        first_s = keep.tile([P, KA * P], U8, name="first_s", align_bytes=64)
        for a in range(KA - 1):
            nc.gpsimd.memset(planes[a][:].bitcast(I32), 0)

        def pick_first(a, c0, c1):
            cols = slice(P * a + c0 // PACK, P * a + c1 // PACK)
            nc.vector.tensor_copy(first_c[:, cols], codes[a][:, c0:c1:PACK])
            nc.vector.tensor_copy(first_s[:, cols], planes[a][:, c0:c1:PACK])

        def pass_first(a):
            cols = slice(P * a, P * (a + 1))
            nc.tensor.matmul_mx(
                out=ya_first[:],
                lhsT=first_c[:, cols].bitcast(FP8X4),
                lhsT_scale=first_s[:, cols],
                rhs=v_w[a][:].bitcast(FP8X4),
                rhs_scale=v_s[a][:],
                start=(a == 0),
                stop=(a == KA - 1),
            )

        for a in range(KA - 1):
            if a > 0:
                cast_wa(0, a, True)
            quant_wa(0, a)
            pick_first(a, 0, KP)
            pass_first(a)
            pass_a(0, a)
        last = KA - 1
        first_bf = woven_bf[2][:, 0:KP]
        nc.vector.tensor_copy(
            first_bf.rearrange("p (m j) -> p m j", j=PACK),
            wa_raw[0, last, 0].rearrange("p (j m t) -> p m j t", j=PACK, t=PACK)[:, :, :, 0],
        )
        nc.vector.quantize_mx(
            out=first_c[:, P * last : P * KA].bitcast(FP8X4), scales=first_s[:, P * last : P * KA], in_=first_bf
        )
        pass_first(last)
        cast_wa(0, last, True)
        quant_wa(0, last)
        pass_a(0, last)
        gain_flat = gain_t[:].rearrange("p b t -> p (b t)")
        h_t, dev = {}, {}
        h_row = ring.tile([P, S], F32, name="h_row", tag="late", bufs=1, align_bytes=64)
        high = wa_raw[0, 0, 0][:, 0:S]
        low = wa_raw[0, 0, 0][:, S : 2 * S]
        nc.vector.tensor_tensor(high, ya_first[:], yb_first[:], ALU.max)
        nc.vector.tensor_tensor(low, ya_first[:], yb_first[:], ALU.min)
        dev[0] = slab(0, [P, PACK, NB], F32, "dev0")
        dev[1] = slab(1, [P, PACK, NB], F32, "dev1")
        half_dif = keep.tile([P, RB * PACK], F32, name="half_dif")
        nc.vector.tensor_scalar(dev[0][:, :, 0], gain_flat[:, 1:5], 0.5, 0.5, ALU.mult, ALU.add)
        nc.vector.tensor_scalar(dev[1][:, 0:3, 0], gain_flat[:, 5:8], 0.5, 0.5, ALU.mult, ALU.add)
        nc.vector.scalar_tensor_tensor(h_row[:], low, gain_flat[:, 0:1], high, ALU.mult, ALU.add)
        nc.vector.tensor_scalar(half_dif[:], gain_flat, -0.5, 0.5, ALU.mult, ALU.add)
        h_t[0] = h_row[:]
        drain_a(0, 1, PACK, False)

        parts, page_bf, x_bf = {}, {}, {}

        def turn(n):
            b, t = divmod(n, PACK)
            dif = bank(4 + 2 * (n % 2), "dif")
            tot = bank(5 + 2 * (n % 2), "tot")
            for first in (True, False):
                for acc, other in ((dif, ybn_t), (tot, yb_t)):
                    for jb in range(JB):
                        cols = slice(P * jb, P * (jb + 1))
                        term = other if first == (n == PACK) else ya_t
                        nc.tensor.matmul(
                            acc[:, cols],
                            term[b, jb][:, t, :],
                            ident[:],
                            start=(first and jb == 0),
                            stop=(not first and jb == JB - 1),
                            is_transpose=True,
                        )
            if n == PACK:
                page_bf[0] = slab(2, [P, T2 * PACK], BF16, "page_bf")
                gap = page_bf[0][:].bitcast(F32)[:, 0:S]
                mid = wa_raw[1, 2, 0][:, S : 2 * S]
            else:
                mid = mids[n % 2][:]
                if n == PACK + 1:
                    gap = page_bf[0][:].bitcast(F32)[:, 2 * S : 3 * S]
                else:
                    gap = gaps[n % 2][:]
            nc.scalar.activation(gap, dif[:], ACT.Abs)
            nc.scalar.activation(mid, tot[:], ACT.Copy, scale=dev[(n - 1) // PACK][:, (n - 1) % PACK, 0:1])
            parts[n] = (gap, mid)

        def combine(n):
            gap, mid = parts[n]
            if n < 3:
                h_t[n] = ring.tile([P, S], F32, name="h_two", tag="late", bufs=1, align_bytes=64)[:]
            elif n < 7:
                h_t[n] = wa_bf[1, KA - 1, 0].bitcast(F32)[:, S * (n % 2) : S * (n % 2 + 1)]
            else:
                h_t[n] = page_bf[0][:].bitcast(F32)[:, 2 * S * (n - 6) : 2 * S * (n - 6) + S]
            nc.vector.scalar_tensor_tensor(h_t[n], gap, half_dif[:, n : n + 1], mid, ALU.mult, ALU.add)

        def put(n):
            b, t = divmod(n, PACK)
            nc.vector.tensor_tensor(page[n][:].indirect(idx2[:]), h_t[n], wg[:, S * t : S * (t + 1)], ALU.mult)

        def place(n):
            return n if n < PACK else (1, 2, 0, 1)[n - PACK]

        def join(n):
            t = place(n)
            nc.sync.dma_start(out=comb[:, T2 * t : T2 * (t + 1)], in_=page[n][:])

        def fetch(n, c0=0, c1=NB // 16):
            b, t = divmod(n, PACK)
            cols = slice(16 * c0, 16 * c1)
            nc.vector.tensor_tensor(
                dev[b][:, t, cols], page[n][:].indirect(idx3[:, c0:c1]), base_t[n][:, cols], ALU.subtract
            )

        def x_pair(b, u):
            if b == 0:
                host = wa_raw[1, 2, 0][:, NB * u : NB * (u + 1)]
            else:
                host = comb[:, T2 * (3 - u) : T2 * (3 - u) + NB]
            return host.bitcast(BF16).rearrange("p (t j) -> p t j", t=2)

        def scale_x(n, cols=slice(0, NB)):
            b, t = divmod(n, PACK)
            row = x_pair(b, t // 2)[:, t % 2, cols]
            if n < RB * PACK - 1:
                nc.scalar.activation(row, dev[b][:, t, :], ACT.Copy, scale=metric_t[:, b, t : t + 1])
            else:
                nc.vector.tensor_scalar(row, dev[b][:, t, cols], metric_t[:, b, t : t + 1], None, ALU.mult)

        page_c = [keep.tile([P, T2], U32, name="page_c%d" % b, align_bytes=64) for b in range(RB)]
        page_s = [keep.tile([P, T2], U8, name="page_s%d" % b, align_bytes=64) for b in range(RB)]
        x_c = [keep.tile([P, NB], U32, name="x_c%d" % b, align_bytes=64) for b in range(RB)]
        x_s = [keep.tile([P, NB], U8, name="x_s%d" % b, align_bytes=64) for b in range(RB)]

        def weave_page(b, t0=0, t1=PACK, halves=(0, 1)):
            if t0 == 0 and b == 1:
                page_bf[b] = slab(3, [P, T2 * PACK], BF16, "page_bf")
            for u in halves:
                cols = slice(512 * u, 512 * (u + 1))
                if b == RB - 1 and t1 == PACK:
                    nc.scalar.copy(comb_rows[:, place(RB * PACK - 1), cols], page[RB * PACK - 1][:, cols])
                first = place(PACK * b + t0)
                dst, src = woven(
                    page_bf[b][:].rearrange("p (m t) -> p m t", t=PACK)[:, cols, t0:t1],
                    comb_rows[:, first : first + t1 - t0, cols],
                )
                nc.scalar.copy(dst, src)

        def quant_page(b, halves=(0, 1)):
            for u in halves:
                cols = slice(512 * u, 512 * (u + 1))
                nc.vector.quantize_mx(
                    out=page_c[b][:, cols].bitcast(FP8X4),
                    scales=page_s[b][:, cols],
                    in_=page_bf[b][:, 2048 * u : 2048 * (u + 1)],
                )

        def weave_x(b, t0=0, t1=PACK, cols=slice(0, NB)):
            if t0 == 0:
                x_bf[b] = woven_bf[b][:].rearrange("p (j t) -> p j t", t=PACK)
            if b == 0:
                rows = wa_raw[1, 2, 0][:, 0 : 2 * NB].bitcast(BF16).rearrange("p (t j) -> p t j", t=PACK)
            else:
                rows = x_pair(b, t0 // 2)
            dst, src = woven(x_bf[b][:, cols, t0:t1], rows[:, :, cols])
            if t0 == 0:
                nc.scalar.copy(dst, src)
            else:
                nc.vector.tensor_copy(dst, src)

        def quant_x(b, cols=slice(0, NB)):
            nc.vector.quantize_mx(
                out=x_c[b][:, cols].bitcast(FP8X4),
                scales=x_s[b][:, cols],
                in_=x_bf[b][:, cols, :].rearrange("p w t -> p (w t)"),
            )

        put(0)
        turn(1)
        product_b(1, [0, 1, 2, 3])
        combine(1)
        turn(2)
        cast_wa(1, 0, False)
        fetch(0)
        quant_wa(1, 0)
        pass_a(1, 0)
        put(1)
        combine(2)
        join(0)
        cast_wa(1, 1, False)
        join(1)
        turn(3)
        fetch(1)
        quant_wa(1, 1)
        pass_a(1, 1)
        cast_wa(1, 2, False)
        put(2)
        quant_wa(1, 2)
        pass_a(1, 2)
        drain_a(1, 0, 1, False)
        turn(4)
        drain_a(1, 1, PACK, False)
        join(2)
        scale_x(0)
        scale_x(1)
        combine(3)
        fetch(2)
        put(3)
        join(3)
        turn(5)
        combine(4)
        fetch(3)
        put(4)
        combine(5)
        turn(6)
        scale_x(2)
        scale_x(3)
        weave_page(0, halves=(0,))
        fetch(4)
        weave_page(0, halves=(1,))
        join(4)
        quant_page(0, halves=(0,))
        put(5)
        join(5)
        combine(6)
        turn(7)
        weave_x(0)
        scale_x(4)
        fetch(5)
        scale_x(5)
        quant_page(0, halves=(1,))
        put(6)
        join(6)
        quant_x(0)
        weave_page(1, 0, 2)
        weave_x(1, 0, 2)
        combine(7)
        fetch(6)
        scale_x(6)
        put(7)
        weave_page(1, 2, PACK)
        halves = (slice(0, NB // 2), slice(NB // 2, NB))
        fetch(7, 0, 16)
        fetch(7, 16, 32)
        for cols in halves:
            scale_x(7, cols)
        for cols in halves:
            weave_x(1, 2, PACK, cols)
        for cols in halves:
            quant_x(1, cols)
        quant_page(1, halves=(0,))
        quant_page(1, halves=(1,))

        for i in range(MT):
            acc = bank(i, "score")
            cols = slice(P * i, P * (i + 1))
            for b in range(RB):
                nc.tensor.matmul_mx(
                    out=acc[:],
                    lhsT=page_c[b][:, cols].bitcast(FP8X4),
                    lhsT_scale=page_s[b][:, cols],
                    rhs=x_c[b][:].bitcast(FP8X4),
                    rhs_scale=x_s[b][:],
                    start=(b == 0),
                    stop=(b == RB - 1),
                )
            res = base_t[i]
            nc.scalar.activation(res[:], acc[:], ACT.Tanh, scale=slot_t[:, i : i + 1])
            nc.sync.dma_start(out=out[cols, :], in_=res[:])
